import numpy as np
import ml_dtypes


def mxq(x, axis, fmt="e4m3"):
    dtype, down = {"e4m3": (ml_dtypes.float8_e4m3fn, 7), "e5m2": (ml_dtypes.float8_e5m2, 14)}[fmt]
    v = np.moveaxis(np.asarray(x, np.float32).astype(ml_dtypes.bfloat16).astype(np.float64), axis, -1)
    blocks = v.reshape(v.shape[:-1] + (-1, 32))
    amax = np.abs(blocks).max(-1, keepdims=True)
    byte = np.maximum(np.where(amax > 0, np.frexp(amax)[1] - 1 + 127, 0) - down, 1)
    scale = np.exp2(byte - 127.0)
    codes = (blocks / scale).astype(np.float32).astype(dtype).astype(np.float64)
    return np.moveaxis((codes * scale).reshape(v.shape), -1, axis)


WIDE = False


def mx_kscale(k, group=512):
    if not WIDE:
        return np.ones(k)
    levels = np.array([10, -10, 5, -5, 0])
    if group != 512:
        return np.exp2(np.random.permutation(np.resize(levels, k // group))).repeat(group)
    if k % 512:
        return np.exp2(np.random.permutation(np.resize(levels, k // 32))).repeat(32)
    a = np.empty((k // 512, 16))
    for p in range(k // 512):
        a[p, :8] = np.random.permutation(np.resize(levels, 8))
        for g in range(8):
            far = levels[np.abs(levels - a[p, g]) >= 10]
            a[p, g + 8] = far[np.random.randint(len(far))]
    return np.exp2(a.ravel()).repeat(32)


def f64(x):
    return np.asarray(x).astype(np.float64)


G, D, M, N = 4, 256, 128, 1024


def setup_inputs():
    n = np.random.standard_normal
    s = mx_kscale(D, 0)[:, None]
    return {
        "x": (n((G, D, N)) * s).astype(np.float32),
        "w": (n((G, D, M)) / np.sqrt(D) / s).astype(np.float32),
        "u": (n((G, D, M)) / np.sqrt(D) / s).astype(np.float32),
        "r": n((G, M, N)).astype(np.float32),
    }


def reference(x, w, u, r):
    xq = mxq(f64(x), 1, "e4m3")
    h = mxq(f64(w), 1, "e4m3").transpose(0, 2, 1) @ xq
    g = mxq(f64(u), 1, "e4m3").transpose(0, 2, 1) @ xq
    y = np.tanh(h) * g
    y = y + f64(r)
    return y

@@ -1,0 +1,179 @@
+from contextlib import ExitStack
+
+import concourse.mybir as mybir
+
+G, D, M, N = 4, 256, 128, 1024
+FLOPS = 2 * 2 * G * D * M * N
+
+F32 = mybir.dt.float32
+BF16 = mybir.dt.bfloat16
+U32 = mybir.dt.uint32
+U8 = mybir.dt.uint8
+FP8X4 = mybir.dt.float8_e4m3fn_x4
+ACT = mybir.ActivationFunctionType
+ALU = mybir.AluOpType
+
+P = 128
+PACK = 4
+ROWS = D // PACK
+SIDE = P // ROWS
+HALF = 512
+RUN = 4
+
+
+def tile_rows_gglu_tanh_res_kernel(tc, x, w, u, r, out):
+    nc = tc.nc
+    with ExitStack() as ctx:
+        sb = ctx.enter_context(tc.tile_pool(name="sb", bufs=1))
+        ps = ctx.enter_context(tc.psum_pool(name="ps", bufs=1))
+        ctx.enter_context(tc.manual_schedule())
+
+        units = [(s, h) for s in range(G // SIDE) for h in range(N // HALF)]
+        x_raw = [sb.tile([P, PACK, HALF], F32, name="x_raw%d" % k, align_bytes=64) for k in range(4)]
+        x_bf = [sb.tile([P, HALF, PACK], BF16, name="x_bf%d" % k, align_bytes=64) for k in range(4)]
+        x_code = [sb.tile([P, HALF], U32, name="x_code%d" % k, align_bytes=64) for k in range(4)]
+        x_scale = [sb.tile([P, HALF], U8, name="x_scale%d" % k, align_bytes=64) for k in range(4)]
+        w_raw = [sb.tile([P, 2, PACK, M], F32, name="w_raw%d" % s, align_bytes=64) for s in range(2)]
+        w_bf = [sb.tile([P, 2, M, PACK], BF16, name="w_bf%d" % s, align_bytes=64) for s in range(2)]
+        w_code = [sb.tile([P, 2 * M], U32, name="w_code%d" % s, align_bytes=64) for s in range(2)]
+        w_scale = [sb.tile([P, 2 * M], U8, name="w_scale%d" % s, align_bytes=64) for s in range(2)]
+        gate = [sb.tile([P, SIDE, HALF], F32, name="gate%d" % k, align_bytes=64) for k in range(4)]
+        res = [sb.tile([P, SIDE, HALF], F32, name="res%d" % k, align_bytes=64) for k in range(4)]
+        acc = [[[ps.tile([P, HALF], F32, name="acc%d%d%d" % (b, c, z)) for z in range(2)] for c in range(SIDE)] for b in range(2)]
+        warm = sb.tile([P, 8], F32, name="warm")
+        warm_out = sb.tile([P, 8], F32, name="warm_out")
+
+        def load_x(k, a=0, b=HALF):
+            s, h = units[k]
+            src = x[SIDE * s : SIDE * (s + 1), :, HALF * h + a : HALF * h + b]
+            nc.sync.dma_start(out=x_raw[k][:, :, a:b], in_=src.rearrange("c (p j) n -> (c p) j n", j=PACK))
+
+        def load_w(s, z):
+            src = (w, u)[z][SIDE * s : SIDE * (s + 1)]
+            nc.sync.dma_start(out=w_raw[s][:, z], in_=src.rearrange("c (p j) m -> (c p) j m", j=PACK))
+
+        def load_r(k):
+            s, h = units[k]
+            src = r[SIDE * s : SIDE * (s + 1), :, HALF * h : HALF * (h + 1)]
+            nc.sync.dma_start(out=res[k][:], in_=src.rearrange("c m n -> m c n"))
+
+        def interleave(on_vector, dst, src):
+            d = dst.rearrange("p (c i) j -> p c j i", i=RUN)
+            v = src.rearrange("p j (c i) -> p c j i", i=RUN)
+            if on_vector:
+                nc.vector.tensor_copy(out=d, in_=v)
+            else:
+                nc.scalar.copy(out=d, in_=v)
+
+        def weave_x(k, on_vector, a, b):
+            interleave(on_vector, x_bf[k][:, a:b, :], x_raw[k][:, :, a:b])
+
+        def weave_w(s, z, on_vector):
+            interleave(on_vector, w_bf[s][:, z], w_raw[s][:, z])
+
+        def quant_x(k, a=0, b=HALF):
+            nc.vector.quantize_mx(
+                out=x_code[k][:, a:b].bitcast(FP8X4),
+                scales=x_scale[k][:, a:b],
+                in_=x_bf[k][:, a:b, :].rearrange("p n j -> p (n j)"),
+            )
+
+        def quant_w(s):
+            nc.vector.quantize_mx(
+                out=w_code[s][:].bitcast(FP8X4),
+                scales=w_scale[s][:],
+                in_=w_bf[s][:].rearrange("p z m j -> p (z m j)"),
+            )
+
+        def multiply(k):
+            s = units[k][0]
+            for z in range(2):
+                for c in range(SIDE):
+                    rows = slice(ROWS * c, ROWS * (c + 1))
+                    cols = slice(M * z, M * (z + 1))
+                    nc.tensor.matmul_mx(
+                        out=acc[k % 2][c][z][:],
+                        lhsT=w_code[s][rows, cols].bitcast(FP8X4),
+                        lhsT_scale=w_scale[s][rows, cols],
+                        rhs=x_code[k][rows, :].bitcast(FP8X4),
+                        rhs_scale=x_scale[k][rows, :],
+                        start=True,
+                        stop=True,
+                    )
+
+        def activate(k, c, a=0, b=HALF):
+            nc.scalar.activation(out=gate[k][:, c, a:b], in_=acc[k % 2][c][0][:, a:b], func=ACT.Tanh)
+
+        def product(k, c, a=0, b=HALF):
+            nc.vector.tensor_tensor(out=gate[k][:, c, a:b], in0=gate[k][:, c, a:b], in1=acc[k % 2][c][1][:, a:b], op=ALU.mult)
+
+        def residual(k, c0=0, c1=SIDE, a=0, b=HALF):
+            nc.vector.tensor_tensor(out=res[k][:, c0:c1, a:b], in0=gate[k][:, c0:c1, a:b], in1=res[k][:, c0:c1, a:b], op=ALU.add)
+
+        def store(k, c0=0, c1=SIDE, a=0, b=HALF):
+            s, h = units[k]
+            dst = out[SIDE * s + c0 : SIDE * s + c1, :, HALF * h + a : HALF * h + b]
+            nc.sync.dma_start(out=dst.rearrange("c m n -> m c n"), in_=res[k][:, c0:c1, a:b])
+
+        load_x(0)
+        load_w(0, 0)
+        load_w(0, 1)
+        load_x(1)
+        load_w(1, 0)
+        load_w(1, 1)
+        load_x(2)
+        load_r(0)
+        load_x(3)
+        load_r(1)
+        load_r(2)
+        load_r(3)
+        nc.vector.memset(warm[:], 0.0)
+        nc.scalar.activation(out=warm_out[:], in_=warm[:], func=ACT.Tanh)
+        weave_x(0, True, 0, 320)
+        weave_x(0, False, 320, 512)
+        weave_w(0, 0, True)
+        quant_x(0)
+        weave_w(0, 1, False)
+        quant_w(0)
+        multiply(0)
+        activate(0, 0)
+        activate(0, 1)
+        product(0, 0)
+        weave_x(1, True, 0, 256)
+        weave_x(1, False, 256, 512)
+        product(0, 1)
+        weave_w(1, 0, True)
+        weave_w(1, 1, False)
+        quant_x(1)
+        quant_w(1)
+        multiply(1)
+        activate(1, 0)
+        activate(1, 1)
+        product(1, 0)
+        weave_x(2, True, 0, 256)
+        weave_x(2, False, 256, 512)
+        product(1, 1)
+        quant_x(2)
+        multiply(2)
+        residual(0)
+        activate(2, 0)
+        activate(2, 1)
+        product(2, 0)
+        weave_x(3, True, 0, 256)
+        weave_x(3, False, 256, 512)
+        product(2, 1)
+        quant_x(3)
+        multiply(3)
+        residual(1)
+        activate(3, 0)
+        activate(3, 1)
+        residual(2)
+        product(3, 0)
+        product(3, 1)
+        residual(3, 0, 1)
+        residual(3, 1, 2)
+        store(0)
+        store(1)
+        store(2)
+        store(3, 0, 1)
+        store(3, 1, 2)

@@ -17,6 +17,7 @@ P = 128
 PACK = 4
 ROWS = D // PACK
 SIDE = P // ROWS
+PAIRS = G // SIDE
 HALF = 512
 RUN = 4
 
@@ -28,54 +29,57 @@ def tile_rows_gglu_tanh_res_kernel(tc, x, w, u, r, out):
         ps = ctx.enter_context(tc.psum_pool(name="ps", bufs=1))
         ctx.enter_context(tc.manual_schedule())
 
-        units = [(s, h) for s in range(G // SIDE) for h in range(N // HALF)]
-        x_raw = [sb.tile([P, PACK, HALF], F32, name="x_raw%d" % k, align_bytes=64) for k in range(4)]
-        x_bf = [sb.tile([P, HALF, PACK], BF16, name="x_bf%d" % k, align_bytes=64) for k in range(4)]
-        x_code = [sb.tile([P, HALF], U32, name="x_code%d" % k, align_bytes=64) for k in range(4)]
-        x_scale = [sb.tile([P, HALF], U8, name="x_scale%d" % k, align_bytes=64) for k in range(4)]
-        w_raw = [sb.tile([P, 2, PACK, M], F32, name="w_raw%d" % s, align_bytes=64) for s in range(2)]
-        w_bf = [sb.tile([P, 2, M, PACK], BF16, name="w_bf%d" % s, align_bytes=64) for s in range(2)]
-        w_code = [sb.tile([P, 2 * M], U32, name="w_code%d" % s, align_bytes=64) for s in range(2)]
-        w_scale = [sb.tile([P, 2 * M], U8, name="w_scale%d" % s, align_bytes=64) for s in range(2)]
-        gate = [sb.tile([P, SIDE, HALF], F32, name="gate%d" % k, align_bytes=64) for k in range(4)]
-        res = [sb.tile([P, SIDE, HALF], F32, name="res%d" % k, align_bytes=64) for k in range(4)]
-        acc = [[[ps.tile([P, HALF], F32, name="acc%d%d%d" % (b, c, z)) for z in range(2)] for c in range(SIDE)] for b in range(2)]
+        def tiles(name, shape, dtype):
+            return [sb.tile(shape, dtype, name="%s%d" % (name, s), align_bytes=64) for s in range(PAIRS)]
+
+        x_raw = tiles("x_raw", [P, PACK, N], F32)
+        x_bf = tiles("x_bf", [P, N, PACK], BF16)
+        x_code = tiles("x_code", [P, N], U32)
+        x_scale = tiles("x_scale", [P, N], U8)
+        w_raw = tiles("w_raw", [P, 2, PACK, M], F32)
+        w_bf = tiles("w_bf", [P, 2, M, PACK], BF16)
+        w_code = tiles("w_code", [P, 2 * M], U32)
+        w_scale = tiles("w_scale", [P, 2 * M], U8)
+        gate = tiles("gate", [P, SIDE, N], F32)
+        res = tiles("res", [P, SIDE, N], F32)
+        acc = [[[ps.tile([P, HALF], F32, name="acc%d%d%d" % (h, c, z)) for z in range(2)] for c in range(SIDE)] for h in range(2)]
         warm = sb.tile([P, 8], F32, name="warm")
         warm_out = sb.tile([P, 8], F32, name="warm_out")
 
-        def load_x(k, a=0, b=HALF):
-            s, h = units[k]
-            src = x[SIDE * s : SIDE * (s + 1), :, HALF * h + a : HALF * h + b]
-            nc.sync.dma_start(out=x_raw[k][:, :, a:b], in_=src.rearrange("c (p j) n -> (c p) j n", j=PACK))
+        def load_x(s, a, b):
+            src = x[SIDE * s : SIDE * (s + 1), :, a:b]
+            nc.sync.dma_start(out=x_raw[s][:, :, a:b], in_=src.rearrange("c (p j) n -> (c p) j n", j=PACK))
 
         def load_w(s, z):
             src = (w, u)[z][SIDE * s : SIDE * (s + 1)]
             nc.sync.dma_start(out=w_raw[s][:, z], in_=src.rearrange("c (p j) m -> (c p) j m", j=PACK))
 
-        def load_r(k):
-            s, h = units[k]
-            src = r[SIDE * s : SIDE * (s + 1), :, HALF * h : HALF * (h + 1)]
-            nc.sync.dma_start(out=res[k][:], in_=src.rearrange("c m n -> m c n"))
+        def load_r(s, c0, c1, a, b):
+            src = r[SIDE * s + c0 : SIDE * s + c1, :, a:b]
+            nc.sync.dma_start(out=res[s][:, c0:c1, a:b], in_=src.rearrange("c m n -> m c n"))
 
-        def interleave(on_vector, dst, src):
+        def interleave(e, dst, src):
             d = dst.rearrange("p (c i) j -> p c j i", i=RUN)
             v = src.rearrange("p j (c i) -> p c j i", i=RUN)
-            if on_vector:
+            if e == "V":
                 nc.vector.tensor_copy(out=d, in_=v)
+            elif e == "G":
+                nc.gpsimd.tensor_scalar(out=d, in0=v, scalar1=1.0, scalar2=0.0, op0=ALU.mult, op1=ALU.add)
             else:
                 nc.scalar.copy(out=d, in_=v)
 
-        def weave_x(k, on_vector, a, b):
-            interleave(on_vector, x_bf[k][:, a:b, :], x_raw[k][:, :, a:b])
+        def weave_x(e, s, a, b):
+            interleave(e, x_bf[s][:, a:b, :], x_raw[s][:, :, a:b])
 
-        def weave_w(s, z, on_vector):
-            interleave(on_vector, w_bf[s][:, z], w_raw[s][:, z])
+        def weave_w(e, s, z):
+            interleave(e, w_bf[s][:, z], w_raw[s][:, z])
 
-        def quant_x(k, a=0, b=HALF):
+        def quant_x(s, h):
+            cols = slice(HALF * h, HALF * (h + 1))
             nc.vector.quantize_mx(
-                out=x_code[k][:, a:b].bitcast(FP8X4),
-                scales=x_scale[k][:, a:b],
-                in_=x_bf[k][:, a:b, :].rearrange("p n j -> p (n j)"),
+                out=x_code[s][:, cols].bitcast(FP8X4),
+                scales=x_scale[s][:, cols],
+                in_=x_bf[s][:, cols, :].rearrange("p n j -> p (n j)"),
             )
 
         def quant_w(s):
@@ -85,95 +89,96 @@ def tile_rows_gglu_tanh_res_kernel(tc, x, w, u, r, out):
                 in_=w_bf[s][:].rearrange("p z m j -> p (z m j)"),
             )
 
-        def multiply(k):
-            s = units[k][0]
+        def multiply(s, h):
+            cols = slice(HALF * h, HALF * (h + 1))
             for z in range(2):
                 for c in range(SIDE):
                     rows = slice(ROWS * c, ROWS * (c + 1))
-                    cols = slice(M * z, M * (z + 1))
+                    outs = slice(M * z, M * (z + 1))
                     nc.tensor.matmul_mx(
-                        out=acc[k % 2][c][z][:],
-                        lhsT=w_code[s][rows, cols].bitcast(FP8X4),
-                        lhsT_scale=w_scale[s][rows, cols],
-                        rhs=x_code[k][rows, :].bitcast(FP8X4),
-                        rhs_scale=x_scale[k][rows, :],
+                        out=acc[h][c][z][:],
+                        lhsT=w_code[s][rows, outs].bitcast(FP8X4),
+                        lhsT_scale=w_scale[s][rows, outs],
+                        rhs=x_code[s][rows, cols].bitcast(FP8X4),
+                        rhs_scale=x_scale[s][rows, cols],
                         start=True,
                         stop=True,
                     )
 
-        def activate(k, c, a=0, b=HALF):
-            nc.scalar.activation(out=gate[k][:, c, a:b], in_=acc[k % 2][c][0][:, a:b], func=ACT.Tanh)
+        def activate(s, h, c):
+            nc.scalar.activation(out=gate[s][:, c, HALF * h : HALF * (h + 1)], in_=acc[h][c][0][:], func=ACT.Tanh)
 
-        def product(k, c, a=0, b=HALF):
-            nc.vector.tensor_tensor(out=gate[k][:, c, a:b], in0=gate[k][:, c, a:b], in1=acc[k % 2][c][1][:, a:b], op=ALU.mult)
+        def product(s, h, c):
+            t = gate[s][:, c, HALF * h : HALF * (h + 1)]
+            nc.vector.tensor_tensor(out=t, in0=t, in1=acc[h][c][1][:], op=ALU.mult)
 
-        def residual(k, c0=0, c1=SIDE, a=0, b=HALF):
-            nc.vector.tensor_tensor(out=res[k][:, c0:c1, a:b], in0=gate[k][:, c0:c1, a:b], in1=res[k][:, c0:c1, a:b], op=ALU.add)
+        def residual(e, s, c, a, b):
+            eng = nc.vector if e == "V" else nc.gpsimd
+            eng.tensor_tensor(out=res[s][:, c, a:b], in0=gate[s][:, c, a:b], in1=res[s][:, c, a:b], op=ALU.add)
 
-        def store(k, c0=0, c1=SIDE, a=0, b=HALF):
-            s, h = units[k]
-            dst = out[SIDE * s + c0 : SIDE * s + c1, :, HALF * h + a : HALF * h + b]
-            nc.sync.dma_start(out=dst.rearrange("c m n -> m c n"), in_=res[k][:, c0:c1, a:b])
+        def store(s, c, a, b):
+            nc.sync.dma_start(out=out[SIDE * s + c, :, a:b], in_=res[s][:, c, a:b])
 
-        load_x(0)
+        load_x(0, 0, 1024)
         load_w(0, 0)
         load_w(0, 1)
-        load_x(1)
+        load_x(1, 0, 512)
         load_w(1, 0)
         load_w(1, 1)
-        load_x(2)
-        load_r(0)
-        load_x(3)
-        load_r(1)
-        load_r(2)
-        load_r(3)
+        load_x(1, 512, 1024)
+        load_r(0, 0, 1, 0, 1024)
+        load_r(0, 1, 2, 0, 1024)
+        load_r(1, 0, 2, 0, 512)
+        load_r(1, 0, 2, 512, 1024)
         nc.vector.memset(warm[:], 0.0)
         nc.scalar.activation(out=warm_out[:], in_=warm[:], func=ACT.Tanh)
-        weave_x(0, True, 0, 320)
-        weave_x(0, False, 320, 512)
-        weave_w(0, 0, True)
-        quant_x(0)
-        weave_w(0, 1, False)
+        weave_x("V", 0, 0, 512)
+        weave_x("S", 0, 512, 1024)
+        weave_w("V", 0, 0)
+        weave_w("V", 0, 1)
+        quant_x(0, 0)
         quant_w(0)
-        multiply(0)
-        activate(0, 0)
-        activate(0, 1)
-        product(0, 0)
-        weave_x(1, True, 0, 256)
-        weave_x(1, False, 256, 512)
-        product(0, 1)
-        weave_w(1, 0, True)
-        weave_w(1, 1, False)
-        quant_x(1)
+        quant_x(0, 1)
+        multiply(0, 0)
+        multiply(0, 1)
+        weave_x("V", 1, 0, 256)
+        weave_x("S", 1, 256, 512)
+        weave_w("V", 1, 0)
+        weave_w("V", 1, 1)
+        quant_x(1, 0)
+        activate(0, 0, 0)
+        activate(0, 0, 1)
+        activate(0, 1, 0)
+        product(0, 0, 0)
         quant_w(1)
-        multiply(1)
-        activate(1, 0)
-        activate(1, 1)
-        product(1, 0)
-        weave_x(2, True, 0, 256)
-        weave_x(2, False, 256, 512)
-        product(1, 1)
-        quant_x(2)
-        multiply(2)
-        residual(0)
-        activate(2, 0)
-        activate(2, 1)
-        product(2, 0)
-        weave_x(3, True, 0, 256)
-        weave_x(3, False, 256, 512)
-        product(2, 1)
-        quant_x(3)
-        multiply(3)
-        residual(1)
-        activate(3, 0)
-        activate(3, 1)
-        residual(2)
-        product(3, 0)
-        product(3, 1)
-        residual(3, 0, 1)
-        residual(3, 1, 2)
-        store(0)
-        store(1)
-        store(2)
-        store(3, 0, 1)
-        store(3, 1, 2)
+        product(0, 0, 1)
+        multiply(1, 0)
+        product(0, 1, 0)
+        activate(0, 1, 1)
+        weave_x("V", 1, 512, 640)
+        weave_x("S", 1, 640, 1024)
+        residual("V", 0, 0, 0, 1024)
+        quant_x(1, 1)
+        product(0, 1, 1)
+        multiply(1, 1)
+        activate(1, 0, 0)
+        activate(1, 0, 1)
+        activate(1, 1, 0)
+        activate(1, 1, 1)
+        residual("V", 0, 1, 0, 512)
+        residual("G", 0, 1, 512, 1024)
+        product(1, 0, 0)
+        product(1, 0, 1)
+        residual("G", 1, 0, 0, 512)
+        product(1, 1, 0)
+        product(1, 1, 1)
+        residual("V", 1, 1, 0, 512)
+        residual("V", 1, 0, 512, 1024)
+        residual("V", 1, 1, 512, 1024)
+        store(0, 0, 0, 1024)
+        store(0, 1, 0, 512)
+        store(0, 1, 512, 1024)
+        store(1, 0, 0, 512)
+        store(1, 1, 0, 512)
+        store(1, 0, 512, 1024)
+        store(1, 1, 512, 1024)

@@ -32,7 +32,8 @@ def tile_rows_gglu_tanh_res_kernel(tc, x, w, u, r, out):
         def tiles(name, shape, dtype):
             return [sb.tile(shape, dtype, name="%s%d" % (name, s), align_bytes=64) for s in range(PAIRS)]
 
-        x_raw = tiles("x_raw", [P, PACK, N], F32)
+        XL = [(0, 0, 1024), (1, 0, 512), (1, 512, 1024)]
+        x_raw = [sb.tile([P, PACK, b - a], F32, name="x_raw%d" % i, align_bytes=64) for i, (s, a, b) in enumerate(XL)]
         x_bf = tiles("x_bf", [P, N, PACK], BF16)
         x_code = tiles("x_code", [P, N], U32)
         x_scale = tiles("x_scale", [P, N], U8)
@@ -41,14 +42,25 @@ def tile_rows_gglu_tanh_res_kernel(tc, x, w, u, r, out):
         w_code = tiles("w_code", [P, 2 * M], U32)
         w_scale = tiles("w_scale", [P, 2 * M], U8)
         gate = tiles("gate", [P, SIDE, N], F32)
-        res = tiles("res", [P, SIDE, N], F32)
+        RL = [(0, 0, 1, 0, 1024), (0, 1, 2, 0, 1024), (1, 0, 2, 0, 512), (1, 0, 2, 512, 1024)]
+        res = [sb.tile([P, c1 - c0, b - a], F32, name="res%d" % i, align_bytes=64) for i, (s, c0, c1, a, b) in enumerate(RL)]
         acc = [[[ps.tile([P, HALF], F32, name="acc%d%d%d" % (h, c, z)) for z in range(2)] for c in range(SIDE)] for h in range(2)]
         warm = sb.tile([P, 8], F32, name="warm")
         warm_out = sb.tile([P, 8], F32, name="warm_out")
 
+        def xv(s, a, b):
+            for i, (s2, a2, b2) in enumerate(XL):
+                if s2 == s and a2 <= a and b <= b2:
+                    return x_raw[i][:, :, a - a2 : b - a2]
+
+        def rv(s, c0, c1, a, b):
+            for i, (s2, d0, d1, a2, b2) in enumerate(RL):
+                if s2 == s and a2 <= a and b <= b2 and d0 <= c0 and c1 <= d1:
+                    return res[i][:, c0 - d0 : c1 - d0, a - a2 : b - a2]
+
         def load_x(s, a, b):
             src = x[SIDE * s : SIDE * (s + 1), :, a:b]
-            nc.sync.dma_start(out=x_raw[s][:, :, a:b], in_=src.rearrange("c (p j) n -> (c p) j n", j=PACK))
+            nc.sync.dma_start(out=xv(s, a, b), in_=src.rearrange("c (p j) n -> (c p) j n", j=PACK))
 
         def load_w(s, z):
             src = (w, u)[z][SIDE * s : SIDE * (s + 1)]
@@ -56,7 +68,7 @@ def tile_rows_gglu_tanh_res_kernel(tc, x, w, u, r, out):
 
         def load_r(s, c0, c1, a, b):
             src = r[SIDE * s + c0 : SIDE * s + c1, :, a:b]
-            nc.sync.dma_start(out=res[s][:, c0:c1, a:b], in_=src.rearrange("c m n -> m c n"))
+            nc.sync.dma_start(out=rv(s, c0, c1, a, b), in_=src.rearrange("c m n -> m c n"))
 
         def interleave(e, dst, src):
             d = dst.rearrange("p (c i) j -> p c j i", i=RUN)
@@ -69,7 +81,7 @@ def tile_rows_gglu_tanh_res_kernel(tc, x, w, u, r, out):
                 nc.scalar.copy(out=d, in_=v)
 
         def weave_x(e, s, a, b):
-            interleave(e, x_bf[s][:, a:b, :], x_raw[s][:, :, a:b])
+            interleave(e, x_bf[s][:, a:b, :], xv(s, a, b))
 
         def weave_w(e, s, z):
             interleave(e, w_bf[s][:, z], w_raw[s][:, z])
@@ -114,10 +126,11 @@ def tile_rows_gglu_tanh_res_kernel(tc, x, w, u, r, out):
 
         def residual(e, s, c, a, b):
             eng = nc.vector if e == "V" else nc.gpsimd
-            eng.tensor_tensor(out=res[s][:, c, a:b], in0=gate[s][:, c, a:b], in1=res[s][:, c, a:b], op=ALU.add)
+            t = rv(s, c, c + 1, a, b)[:, 0, :]
+            eng.tensor_tensor(out=t, in0=gate[s][:, c, a:b], in1=t, op=ALU.add)
 
         def store(s, c, a, b):
-            nc.sync.dma_start(out=out[SIDE * s + c, :, a:b], in_=res[s][:, c, a:b])
+            nc.sync.dma_start(out=out[SIDE * s + c, :, a:b], in_=rv(s, c, c + 1, a, b)[:, 0, :])
 
         load_x(0, 0, 1024)
         load_w(0, 0)

@@ -30,23 +30,21 @@ def tile_rows_gglu_tanh_res_kernel(tc, x, w, u, r, out):
         ctx.enter_context(tc.manual_schedule())
 
         def tiles(name, shape, dtype):
-            return [sb.tile(shape, dtype, name="%s%d" % (name, s), align_bytes=64) for s in range(PAIRS)]
+            return [sb.tile(shape, dtype, name="%s%d" % (name, s), align_bytes=64) for s in range(2)]
 
-        XL = [(0, 0, 1024), (1, 0, 512), (1, 512, 1024)]
+        XL = [(0, 0, 512), (0, 512, 1024), (1, 0, 512), (1, 512, 1024)]
         x_raw = [sb.tile([P, PACK, b - a], F32, name="x_raw%d" % i, align_bytes=64) for i, (s, a, b) in enumerate(XL)]
         x_bf = tiles("x_bf", [P, N, PACK], BF16)
         x_code = tiles("x_code", [P, N], U32)
         x_scale = tiles("x_scale", [P, N], U8)
-        w_raw = tiles("w_raw", [P, 2, PACK, M], F32)
+        w_raw = [[sb.tile([P, PACK, M], F32, name="w_raw%d%d" % (s, z), align_bytes=64) for z in range(2)] for s in range(PAIRS)]
         w_bf = tiles("w_bf", [P, 2, M, PACK], BF16)
         w_code = tiles("w_code", [P, 2 * M], U32)
         w_scale = tiles("w_scale", [P, 2 * M], U8)
         gate = tiles("gate", [P, SIDE, N], F32)
-        RL = [(0, 0, 1, 0, 1024), (0, 1, 2, 0, 1024), (1, 0, 2, 0, 512), (1, 0, 2, 512, 1024)]
+        RL = [(0, 0, 1, 0, 1024), (0, 1, 2, 0, 1024), (1, 0, 1, 0, 1024), (1, 1, 2, 0, 1024)]
         res = [sb.tile([P, c1 - c0, b - a], F32, name="res%d" % i, align_bytes=64) for i, (s, c0, c1, a, b) in enumerate(RL)]
         acc = [[[ps.tile([P, HALF], F32, name="acc%d%d%d" % (h, c, z)) for z in range(2)] for c in range(SIDE)] for h in range(2)]
-        warm = sb.tile([P, 8], F32, name="warm")
-        warm_out = sb.tile([P, 8], F32, name="warm_out")
 
         def xv(s, a, b):
             for i, (s2, a2, b2) in enumerate(XL):
@@ -64,7 +62,7 @@ def tile_rows_gglu_tanh_res_kernel(tc, x, w, u, r, out):
 
         def load_w(s, z):
             src = (w, u)[z][SIDE * s : SIDE * (s + 1)]
-            nc.sync.dma_start(out=w_raw[s][:, z], in_=src.rearrange("c (p j) m -> (c p) j m", j=PACK))
+            nc.sync.dma_start(out=w_raw[s][z][:], in_=src.rearrange("c (p j) m -> (c p) j m", j=PACK))
 
         def load_r(s, c0, c1, a, b):
             src = r[SIDE * s + c0 : SIDE * s + c1, :, a:b]
@@ -75,8 +73,6 @@ def tile_rows_gglu_tanh_res_kernel(tc, x, w, u, r, out):
             v = src.rearrange("p j (c i) -> p c j i", i=RUN)
             if e == "V":
                 nc.vector.tensor_copy(out=d, in_=v)
-            elif e == "G":
-                nc.gpsimd.tensor_scalar(out=d, in0=v, scalar1=1.0, scalar2=0.0, op0=ALU.mult, op1=ALU.add)
             else:
                 nc.scalar.copy(out=d, in_=v)
 
@@ -84,7 +80,7 @@ def tile_rows_gglu_tanh_res_kernel(tc, x, w, u, r, out):
             interleave(e, x_bf[s][:, a:b, :], xv(s, a, b))
 
         def weave_w(e, s, z):
-            interleave(e, w_bf[s][:, z], w_raw[s][:, z])
+            interleave(e, w_bf[s][:, z], w_raw[s][z][:])
 
         def quant_x(s, h):
             cols = slice(HALF * h, HALF * (h + 1))
@@ -94,104 +90,112 @@ def tile_rows_gglu_tanh_res_kernel(tc, x, w, u, r, out):
                 in_=x_bf[s][:, cols, :].rearrange("p n j -> p (n j)"),
             )
 
-        def quant_w(s):
+        def quant_w(s, z):
+            outs = slice(M * z, M * (z + 1))
             nc.vector.quantize_mx(
-                out=w_code[s][:].bitcast(FP8X4),
-                scales=w_scale[s][:],
-                in_=w_bf[s][:].rearrange("p z m j -> p (z m j)"),
+                out=w_code[s][:, outs].bitcast(FP8X4),
+                scales=w_scale[s][:, outs],
+                in_=w_bf[s][:, z].rearrange("p m j -> p (m j)"),
             )
 
-        def multiply(s, h):
+        def multiply(s, h, z):
             cols = slice(HALF * h, HALF * (h + 1))
-            for z in range(2):
-                for c in range(SIDE):
-                    rows = slice(ROWS * c, ROWS * (c + 1))
-                    outs = slice(M * z, M * (z + 1))
-                    nc.tensor.matmul_mx(
-                        out=acc[h][c][z][:],
-                        lhsT=w_code[s][rows, outs].bitcast(FP8X4),
-                        lhsT_scale=w_scale[s][rows, outs],
-                        rhs=x_code[s][rows, cols].bitcast(FP8X4),
-                        rhs_scale=x_scale[s][rows, cols],
-                        start=True,
-                        stop=True,
-                    )
+            outs = slice(M * z, M * (z + 1))
+            for c in range(SIDE):
+                rows = slice(ROWS * c, ROWS * (c + 1))
+                nc.tensor.matmul_mx(
+                    out=acc[h][c][z][:],
+                    lhsT=w_code[s][rows, outs].bitcast(FP8X4),
+                    lhsT_scale=w_scale[s][rows, outs],
+                    rhs=x_code[s][rows, cols].bitcast(FP8X4),
+                    rhs_scale=x_scale[s][rows, cols],
+                    start=True,
+                    stop=True,
+                )
 
         def activate(s, h, c):
             nc.scalar.activation(out=gate[s][:, c, HALF * h : HALF * (h + 1)], in_=acc[h][c][0][:], func=ACT.Tanh)
 
-        def product(s, h, c):
-            t = gate[s][:, c, HALF * h : HALF * (h + 1)]
-            nc.vector.tensor_tensor(out=t, in0=t, in1=acc[h][c][1][:], op=ALU.mult)
+        def product(s, h, c, a=0, b=HALF):
+            t = gate[s][:, c, HALF * h + a : HALF * h + b]
+            nc.vector.tensor_tensor(out=t, in0=t, in1=acc[h][c][1][:, a:b], op=ALU.mult)
 
-        def residual(e, s, c, a, b):
+        def residual(e, s, c0, c1, a, b):
             eng = nc.vector if e == "V" else nc.gpsimd
-            t = rv(s, c, c + 1, a, b)[:, 0, :]
-            eng.tensor_tensor(out=t, in0=gate[s][:, c, a:b], in1=t, op=ALU.add)
+            t = rv(s, c0, c1, a, b)
+            eng.tensor_tensor(out=t, in0=gate[s][:, c0:c1, a:b], in1=t, op=ALU.add)
 
-        def store(s, c, a, b):
-            nc.sync.dma_start(out=out[SIDE * s + c, :, a:b], in_=rv(s, c, c + 1, a, b)[:, 0, :])
+        def store(s, c0, c1, a, b):
+            dst = out[SIDE * s + c0 : SIDE * s + c1, :, a:b]
+            nc.sync.dma_start(out=dst.rearrange("c m n -> m c n"), in_=rv(s, c0, c1, a, b))
 
-        load_x(0, 0, 1024)
+        load_x(0, 0, 512)
         load_w(0, 0)
         load_w(0, 1)
+        load_x(0, 512, 1024)
         load_x(1, 0, 512)
         load_w(1, 0)
         load_w(1, 1)
-        load_x(1, 512, 1024)
         load_r(0, 0, 1, 0, 1024)
+        load_x(1, 512, 1024)
         load_r(0, 1, 2, 0, 1024)
-        load_r(1, 0, 2, 0, 512)
-        load_r(1, 0, 2, 512, 1024)
-        nc.vector.memset(warm[:], 0.0)
-        nc.scalar.activation(out=warm_out[:], in_=warm[:], func=ACT.Tanh)
-        weave_x("V", 0, 0, 512)
-        weave_x("S", 0, 512, 1024)
+        load_r(1, 0, 1, 0, 1024)
+        load_r(1, 1, 2, 0, 1024)
+        weave_x("V", 0, 0, 352)
+        weave_x("S", 0, 352, 512)
         weave_w("V", 0, 0)
-        weave_w("V", 0, 1)
         quant_x(0, 0)
-        quant_w(0)
-        quant_x(0, 1)
-        multiply(0, 0)
-        multiply(0, 1)
-        weave_x("V", 1, 0, 256)
-        weave_x("S", 1, 256, 512)
-        weave_w("V", 1, 0)
-        weave_w("V", 1, 1)
-        quant_x(1, 0)
+        weave_w("S", 0, 1)
+        quant_w(0, 0)
+        quant_w(0, 1)
+        multiply(0, 0, 0)
+        multiply(0, 0, 1)
         activate(0, 0, 0)
+        weave_x("V", 0, 512, 864)
+        weave_x("S", 0, 864, 1024)
         activate(0, 0, 1)
-        activate(0, 1, 0)
         product(0, 0, 0)
-        quant_w(1)
+        quant_x(0, 1)
         product(0, 0, 1)
-        multiply(1, 0)
-        product(0, 1, 0)
+        multiply(0, 1, 0)
+        multiply(0, 1, 1)
+        weave_x("V", 1, 0, 384)
+        weave_x("S", 1, 384, 512)
+        weave_w("S", 1, 0)
+        weave_w("S", 1, 1)
+        quant_x(1, 0)
+        quant_w(1, 0)
+        multiply(1, 0, 0)
+        quant_w(1, 1)
+        multiply(1, 0, 1)
+        activate(0, 1, 0)
         activate(0, 1, 1)
-        weave_x("V", 1, 512, 640)
-        weave_x("S", 1, 640, 1024)
-        residual("V", 0, 0, 0, 1024)
-        quant_x(1, 1)
-        product(0, 1, 1)
-        multiply(1, 1)
+        residual("V", 0, 0, 1, 0, 512)
+        product(0, 1, 0)
+        residual("G", 0, 0, 1, 512, 1024)
         activate(1, 0, 0)
         activate(1, 0, 1)
+        product(0, 1, 1)
+        product(1, 0, 0)
+        product(1, 0, 1, 0, 448)
+        weave_x("V", 1, 512, 784)
+        weave_x("S", 1, 784, 1024)
+        quant_x(1, 1)
+        multiply(1, 1, 0)
+        multiply(1, 1, 1)
         activate(1, 1, 0)
         activate(1, 1, 1)
-        residual("V", 0, 1, 0, 512)
-        residual("G", 0, 1, 512, 1024)
-        product(1, 0, 0)
-        product(1, 0, 1)
-        residual("G", 1, 0, 0, 512)
+        residual("V", 0, 1, 2, 0, 1024)
+        product(1, 0, 1, 448, 512)
+        residual("V", 1, 0, 1, 0, 512)
+        residual("G", 1, 1, 2, 0, 512)
         product(1, 1, 0)
         product(1, 1, 1)
-        residual("V", 1, 1, 0, 512)
-        residual("V", 1, 0, 512, 1024)
-        residual("V", 1, 1, 512, 1024)
-        store(0, 0, 0, 1024)
-        store(0, 1, 0, 512)
-        store(0, 1, 512, 1024)
-        store(1, 0, 0, 512)
-        store(1, 1, 0, 512)
-        store(1, 0, 512, 1024)
-        store(1, 1, 512, 1024)
+        residual("V", 1, 0, 1, 512, 1024)
+        residual("V", 1, 1, 2, 512, 1024)
+        store(0, 0, 1, 0, 1024)
+        store(0, 1, 2, 0, 1024)
+        store(1, 0, 1, 0, 512)
+        store(1, 1, 2, 0, 512)
+        store(1, 0, 1, 512, 1024)
+        store(1, 1, 2, 512, 1024)

@@ -32,7 +32,7 @@ def tile_rows_gglu_tanh_res_kernel(tc, x, w, u, r, out):
         def tiles(name, shape, dtype):
             return [sb.tile(shape, dtype, name="%s%d" % (name, s), align_bytes=64) for s in range(2)]
 
-        XL = [(0, 0, 512), (0, 512, 1024), (1, 0, 512), (1, 512, 1024)]
+        XL = [(0, 0, 512), (0, 512, 1024), (1, 0, 512), (1, 512, 768), (1, 768, 1024)]
         x_raw = [sb.tile([P, PACK, b - a], F32, name="x_raw%d" % i, align_bytes=64) for i, (s, a, b) in enumerate(XL)]
         x_bf = tiles("x_bf", [P, N, PACK], BF16)
         x_code = tiles("x_code", [P, N], U32)
@@ -42,7 +42,7 @@ def tile_rows_gglu_tanh_res_kernel(tc, x, w, u, r, out):
         w_code = tiles("w_code", [P, 2 * M], U32)
         w_scale = tiles("w_scale", [P, 2 * M], U8)
         gate = tiles("gate", [P, SIDE, N], F32)
-        RL = [(0, 0, 1, 0, 1024), (0, 1, 2, 0, 1024), (1, 0, 1, 0, 1024), (1, 1, 2, 0, 1024)]
+        RL = [(0, 0, 1, 0, 1024), (0, 1, 2, 0, 1024), (1, 0, 2, 0, 512), (1, 0, 2, 512, 1024)]
         res = [sb.tile([P, c1 - c0, b - a], F32, name="res%d" % i, align_bytes=64) for i, (s, c0, c1, a, b) in enumerate(RL)]
         acc = [[[ps.tile([P, HALF], F32, name="acc%d%d%d" % (h, c, z)) for z in range(2)] for c in range(SIDE)] for h in range(2)]
 
@@ -82,8 +82,8 @@ def tile_rows_gglu_tanh_res_kernel(tc, x, w, u, r, out):
         def weave_w(e, s, z):
             interleave(e, w_bf[s][:, z], w_raw[s][z][:])
 
-        def quant_x(s, h):
-            cols = slice(HALF * h, HALF * (h + 1))
+        def quant_x(s, h, a=0, b=HALF):
+            cols = slice(HALF * h + a, HALF * h + b)
             nc.vector.quantize_mx(
                 out=x_code[s][:, cols].bitcast(FP8X4),
                 scales=x_scale[s][:, cols],
@@ -113,8 +113,8 @@ def tile_rows_gglu_tanh_res_kernel(tc, x, w, u, r, out):
                     stop=True,
                 )
 
-        def activate(s, h, c):
-            nc.scalar.activation(out=gate[s][:, c, HALF * h : HALF * (h + 1)], in_=acc[h][c][0][:], func=ACT.Tanh)
+        def activate(s, h, c, a=0, b=HALF):
+            nc.scalar.activation(out=gate[s][:, c, HALF * h + a : HALF * h + b], in_=acc[h][c][0][:, a:b], func=ACT.Tanh)
 
         def product(s, h, c, a=0, b=HALF):
             t = gate[s][:, c, HALF * h + a : HALF * h + b]
@@ -137,10 +137,11 @@ def tile_rows_gglu_tanh_res_kernel(tc, x, w, u, r, out):
         load_w(1, 0)
         load_w(1, 1)
         load_r(0, 0, 1, 0, 1024)
-        load_x(1, 512, 1024)
+        load_x(1, 512, 768)
+        load_x(1, 768, 1024)
         load_r(0, 1, 2, 0, 1024)
-        load_r(1, 0, 1, 0, 1024)
-        load_r(1, 1, 2, 0, 1024)
+        load_r(1, 0, 2, 0, 512)
+        load_r(1, 0, 2, 512, 1024)
         weave_x("V", 0, 0, 352)
         weave_x("S", 0, 352, 512)
         weave_w("V", 0, 0)
@@ -156,41 +157,51 @@ def tile_rows_gglu_tanh_res_kernel(tc, x, w, u, r, out):
         activate(0, 0, 1)
         product(0, 0, 0)
         quant_x(0, 1)
-        product(0, 0, 1)
+        product(0, 0, 1, 0, 256)
         multiply(0, 1, 0)
         multiply(0, 1, 1)
-        weave_x("V", 1, 0, 384)
-        weave_x("S", 1, 384, 512)
+        weave_x("V", 1, 0, 352)
+        weave_x("S", 1, 352, 512)
         weave_w("S", 1, 0)
-        weave_w("S", 1, 1)
+        product(0, 0, 1, 256, 512)
         quant_x(1, 0)
         quant_w(1, 0)
         multiply(1, 0, 0)
-        quant_w(1, 1)
-        multiply(1, 0, 1)
+        weave_w("V", 1, 1)
         activate(0, 1, 0)
         activate(0, 1, 1)
-        residual("V", 0, 0, 1, 0, 512)
-        product(0, 1, 0)
-        residual("G", 0, 0, 1, 512, 1024)
+        product(0, 1, 0, 0, 256)
+        quant_w(1, 1)
+        multiply(1, 0, 1)
+        residual("G", 0, 0, 1, 0, 768)
+        product(0, 1, 0, 256, 512)
+        residual("G", 0, 0, 1, 768, 896)
         activate(1, 0, 0)
         activate(1, 0, 1)
         product(0, 1, 1)
         product(1, 0, 0)
         product(1, 0, 1, 0, 448)
-        weave_x("V", 1, 512, 784)
-        weave_x("S", 1, 784, 1024)
-        quant_x(1, 1)
+        weave_x("S", 1, 512, 672)
+        weave_x("V", 1, 672, 768)
+        weave_x("V", 1, 768, 896)
+        weave_x("S", 1, 896, 1024)
+        quant_x(1, 1, 0, 256)
+        quant_x(1, 1, 256, 512)
+        residual("V", 0, 0, 1, 896, 1024)
         multiply(1, 1, 0)
         multiply(1, 1, 1)
-        activate(1, 1, 0)
-        activate(1, 1, 1)
+        activate(1, 1, 0, 0, 256)
+        activate(1, 1, 0, 256, 512)
+        activate(1, 1, 1, 0, 256)
+        activate(1, 1, 1, 256, 512)
         residual("V", 0, 1, 2, 0, 1024)
         product(1, 0, 1, 448, 512)
         residual("V", 1, 0, 1, 0, 512)
         residual("G", 1, 1, 2, 0, 512)
-        product(1, 1, 0)
-        product(1, 1, 1)
+        product(1, 1, 0, 0, 256)
+        product(1, 1, 0, 256, 512)
+        product(1, 1, 1, 0, 256)
+        product(1, 1, 1, 256, 512)
         residual("V", 1, 0, 1, 512, 1024)
         residual("V", 1, 1, 2, 512, 1024)
         store(0, 0, 1, 0, 1024)

@@ -19,7 +19,7 @@ ROWS = D // PACK
 SIDE = P // ROWS
 PAIRS = G // SIDE
 HALF = 512
-RUN = 4
+RUN = 2
 
 
 def tile_rows_gglu_tanh_res_kernel(tc, x, w, u, r, out):

@@ -32,7 +32,7 @@ def tile_rows_gglu_tanh_res_kernel(tc, x, w, u, r, out):
         def tiles(name, shape, dtype):
             return [sb.tile(shape, dtype, name="%s%d" % (name, s), align_bytes=64) for s in range(2)]
 
-        XL = [(0, 0, 512), (0, 512, 1024), (1, 0, 512), (1, 512, 768), (1, 768, 1024)]
+        XL = [(0, 0, 1024), (1, 0, 512), (1, 512, 768), (1, 768, 1024)]
         x_raw = [sb.tile([P, PACK, b - a], F32, name="x_raw%d" % i, align_bytes=64) for i, (s, a, b) in enumerate(XL)]
         x_bf = tiles("x_bf", [P, N, PACK], BF16)
         x_code = tiles("x_code", [P, N], U32)
@@ -98,10 +98,10 @@ def tile_rows_gglu_tanh_res_kernel(tc, x, w, u, r, out):
                 in_=w_bf[s][:, z].rearrange("p m j -> p (m j)"),
             )
 
-        def multiply(s, h, z):
+        def multiply(s, h, z, places=(0, 1)):
             cols = slice(HALF * h, HALF * (h + 1))
             outs = slice(M * z, M * (z + 1))
-            for c in range(SIDE):
+            for c in places:
                 rows = slice(ROWS * c, ROWS * (c + 1))
                 nc.tensor.matmul_mx(
                     out=acc[h][c][z][:],
@@ -125,14 +125,13 @@ def tile_rows_gglu_tanh_res_kernel(tc, x, w, u, r, out):
             t = rv(s, c0, c1, a, b)
             eng.tensor_tensor(out=t, in0=gate[s][:, c0:c1, a:b], in1=t, op=ALU.add)
 
-        def store(s, c0, c1, a, b):
+        def store(queue, s, c0, c1, a, b):
             dst = out[SIDE * s + c0 : SIDE * s + c1, :, a:b]
-            nc.sync.dma_start(out=dst.rearrange("c m n -> m c n"), in_=rv(s, c0, c1, a, b))
+            queue.dma_start(out=dst.rearrange("c m n -> m c n"), in_=rv(s, c0, c1, a, b))
 
-        load_x(0, 0, 512)
+        load_x(0, 0, 1024)
         load_w(0, 0)
         load_w(0, 1)
-        load_x(0, 512, 1024)
         load_x(1, 0, 512)
         load_w(1, 0)
         load_w(1, 1)
@@ -144,50 +143,50 @@ def tile_rows_gglu_tanh_res_kernel(tc, x, w, u, r, out):
         load_r(1, 0, 2, 512, 1024)
         weave_x("V", 0, 0, 352)
         weave_x("S", 0, 352, 512)
+        weave_x("S", 0, 672, 1024)
         weave_w("V", 0, 0)
         quant_x(0, 0)
-        weave_w("S", 0, 1)
         quant_w(0, 0)
-        quant_w(0, 1)
         multiply(0, 0, 0)
+        weave_w("V", 0, 1)
+        weave_x("V", 0, 512, 672)
+        quant_w(0, 1)
         multiply(0, 0, 1)
-        activate(0, 0, 0)
-        weave_x("V", 0, 512, 864)
-        weave_x("S", 0, 864, 1024)
-        activate(0, 0, 1)
-        product(0, 0, 0)
         quant_x(0, 1)
-        product(0, 0, 1, 0, 256)
         multiply(0, 1, 0)
         multiply(0, 1, 1)
-        weave_x("V", 1, 0, 352)
-        weave_x("S", 1, 352, 512)
+        activate(0, 0, 0)
+        activate(0, 0, 1)
+        weave_x("V", 1, 0, 256)
+        weave_x("V", 1, 256, 400)
+        weave_x("S", 1, 400, 512)
+        quant_x(1, 0, 0, 256)
+        product(0, 0, 1, 0, 256)
+        quant_x(1, 0, 256, 512)
         weave_w("S", 1, 0)
         product(0, 0, 1, 256, 512)
-        quant_x(1, 0)
         quant_w(1, 0)
         multiply(1, 0, 0)
-        weave_w("V", 1, 1)
+        weave_w("S", 1, 1)
         activate(0, 1, 0)
         activate(0, 1, 1)
-        product(0, 1, 0, 0, 256)
+        product(0, 0, 0)
         quant_w(1, 1)
         multiply(1, 0, 1)
-        residual("G", 0, 0, 1, 0, 768)
-        product(0, 1, 0, 256, 512)
-        residual("G", 0, 0, 1, 768, 896)
+        residual("G", 0, 0, 1, 0, 512)
+        product(0, 1, 0)
+        residual("G", 0, 0, 1, 512, 768)
         activate(1, 0, 0)
         activate(1, 0, 1)
         product(0, 1, 1)
         product(1, 0, 0)
         product(1, 0, 1, 0, 448)
-        weave_x("S", 1, 512, 672)
-        weave_x("V", 1, 672, 768)
-        weave_x("V", 1, 768, 896)
-        weave_x("S", 1, 896, 1024)
+        residual("V", 0, 0, 1, 768, 1024)
+        weave_x("S", 1, 512, 768)
+        weave_x("V", 1, 768, 928)
+        weave_x("S", 1, 928, 1024)
         quant_x(1, 1, 0, 256)
         quant_x(1, 1, 256, 512)
-        residual("V", 0, 0, 1, 896, 1024)
         multiply(1, 1, 0)
         multiply(1, 1, 1)
         activate(1, 1, 0, 0, 256)
@@ -204,9 +203,9 @@ def tile_rows_gglu_tanh_res_kernel(tc, x, w, u, r, out):
         product(1, 1, 1, 256, 512)
         residual("V", 1, 0, 1, 512, 1024)
         residual("V", 1, 1, 2, 512, 1024)
-        store(0, 0, 1, 0, 1024)
-        store(0, 1, 2, 0, 1024)
-        store(1, 0, 1, 0, 512)
-        store(1, 1, 2, 0, 512)
-        store(1, 0, 1, 512, 1024)
-        store(1, 1, 2, 512, 1024)
+        store(nc.sync, 0, 0, 1, 0, 1024)
+        store(nc.sync, 0, 1, 2, 0, 1024)
+        store(nc.sync, 1, 0, 1, 0, 512)
+        store(nc.sync, 1, 1, 2, 0, 512)
+        store(nc.sync, 1, 0, 1, 512, 1024)
+        store(nc.sync, 1, 1, 2, 512, 1024)

@@ -19,7 +19,18 @@ ROWS = D // PACK
 SIDE = P // ROWS
 PAIRS = G // SIDE
 HALF = 512
+QUARTER = HALF // 2
 RUN = 2
+
+LOW, HIGH, ALL = (0, 2), (2, 4), (0, 4)
+
+VECTOR_PART = 352
+EARLY_PART = 192
+MIDDLE_PART = 384
+LAST_PART = 160
+EARLY_PRODUCT = 320
+HELD = 64
+GPSIMD_END = HALF + QUARTER
 
 
 def tile_rows_gglu_tanh_res_kernel(tc, x, w, u, r, out):
@@ -29,183 +40,208 @@ def tile_rows_gglu_tanh_res_kernel(tc, x, w, u, r, out):
         ps = ctx.enter_context(tc.psum_pool(name="ps", bufs=1))
         ctx.enter_context(tc.manual_schedule())
 
-        def tiles(name, shape, dtype):
-            return [sb.tile(shape, dtype, name="%s%d" % (name, s), align_bytes=64) for s in range(2)]
+        def per_pair(name, shape, dtype):
+            return [sb.tile(shape, dtype, name="%s%d" % (name, pair), align_bytes=64) for pair in range(PAIRS)]
 
-        XL = [(0, 0, 1024), (1, 0, 512), (1, 512, 768), (1, 768, 1024)]
-        x_raw = [sb.tile([P, PACK, b - a], F32, name="x_raw%d" % i, align_bytes=64) for i, (s, a, b) in enumerate(XL)]
-        x_bf = tiles("x_bf", [P, N, PACK], BF16)
-        x_code = tiles("x_code", [P, N], U32)
-        x_scale = tiles("x_scale", [P, N], U8)
-        w_raw = [[sb.tile([P, PACK, M], F32, name="w_raw%d%d" % (s, z), align_bytes=64) for z in range(2)] for s in range(PAIRS)]
-        w_bf = tiles("w_bf", [P, 2, M, PACK], BF16)
-        w_code = tiles("w_code", [P, 2 * M], U32)
-        w_scale = tiles("w_scale", [P, 2 * M], U8)
-        gate = tiles("gate", [P, SIDE, N], F32)
-        RL = [(0, 0, 1, 0, 1024), (0, 1, 2, 0, 1024), (1, 0, 2, 0, 512), (1, 0, 2, 512, 1024)]
-        res = [sb.tile([P, c1 - c0, b - a], F32, name="res%d" % i, align_bytes=64) for i, (s, c0, c1, a, b) in enumerate(RL)]
-        acc = [[[ps.tile([P, HALF], F32, name="acc%d%d%d" % (h, c, z)) for z in range(2)] for c in range(SIDE)] for h in range(2)]
+        x_loads = [
+            (0, 0, N, LOW),
+            (0, 0, HALF, HIGH),
+            (0, HALF, N, HIGH),
+            (1, 0, HALF, ALL),
+            (1, HALF, HALF + QUARTER, ALL),
+            (1, HALF + QUARTER, N, ALL),
+        ]
+        x_raw = [
+            sb.tile([P, j1 - j0, b - a], F32, name="x_raw%d" % i, align_bytes=64)
+            for i, (pair, a, b, (j0, j1)) in enumerate(x_loads)
+        ]
+        x_bf = per_pair("x_bf", [P, N, PACK], BF16)
+        x_code = per_pair("x_code", [P, N], U32)
+        x_scale = per_pair("x_scale", [P, N], U8)
+        w_raw = [
+            [sb.tile([P, PACK, M], F32, name="w_raw%d%d" % (pair, mat), align_bytes=64) for mat in range(2)]
+            for pair in range(PAIRS)
+        ]
+        w_bf = per_pair("w_bf", [P, 2, M, PACK], BF16)
+        w_code = per_pair("w_code", [P, 2 * M], U32)
+        w_scale = per_pair("w_scale", [P, 2 * M], U8)
+        gate = per_pair("gate", [P, SIDE, N], F32)
+        r_loads = [(0, 1, 0, N), (1, 2, 0, N), (2, 4, 0, HALF), (2, 4, HALF, N)]
+        res = [sb.tile([P, g1 - g0, b - a], F32, name="res%d" % i, align_bytes=64) for i, (g0, g1, a, b) in enumerate(r_loads)]
+        acc = [
+            [[ps.tile([P, HALF], F32, name="acc%d%d%d" % (half, c, mat)) for mat in range(2)] for c in range(SIDE)]
+            for half in range(2)
+        ]
 
-        def xv(s, a, b):
-            for i, (s2, a2, b2) in enumerate(XL):
-                if s2 == s and a2 <= a and b <= b2:
-                    return x_raw[i][:, :, a - a2 : b - a2]
+        def x_view(pair, a, b, places):
+            for loaded, (pair_l, a_l, b_l, places_l) in zip(x_raw, x_loads):
+                if (pair_l, places_l) == (pair, places) and a_l <= a and b <= b_l:
+                    return loaded[:, :, a - a_l : b - a_l]
 
-        def rv(s, c0, c1, a, b):
-            for i, (s2, d0, d1, a2, b2) in enumerate(RL):
-                if s2 == s and a2 <= a and b <= b2 and d0 <= c0 and c1 <= d1:
-                    return res[i][:, c0 - d0 : c1 - d0, a - a2 : b - a2]
+        def res_view(g, a, b):
+            for loaded, (g0, g1, a_l, b_l) in zip(res, r_loads):
+                if g0 <= g < g1 and a_l <= a and b <= b_l:
+                    return loaded[:, g - g0 : g - g0 + 1, a - a_l : b - a_l]
 
-        def load_x(s, a, b):
-            src = x[SIDE * s : SIDE * (s + 1), :, a:b]
-            nc.sync.dma_start(out=xv(s, a, b), in_=src.rearrange("c (p j) n -> (c p) j n", j=PACK))
+        def load_x(i):
+            pair, a, b, (j0, j1) = x_loads[i]
+            src = x[SIDE * pair : SIDE * (pair + 1), :, a:b].rearrange("c (p j) n -> (c p) j n", j=PACK)
+            nc.sync.dma_start(out=x_raw[i][:], in_=src[:, j0:j1, :])
 
-        def load_w(s, z):
-            src = (w, u)[z][SIDE * s : SIDE * (s + 1)]
-            nc.sync.dma_start(out=w_raw[s][z][:], in_=src.rearrange("c (p j) m -> (c p) j m", j=PACK))
+        def load_weights(pair):
+            for mat, weights in enumerate((w, u)):
+                src = weights[SIDE * pair : SIDE * (pair + 1)]
+                nc.sync.dma_start(out=w_raw[pair][mat][:], in_=src.rearrange("c (p j) m -> (c p) j m", j=PACK))
 
-        def load_r(s, c0, c1, a, b):
-            src = r[SIDE * s + c0 : SIDE * s + c1, :, a:b]
-            nc.sync.dma_start(out=rv(s, c0, c1, a, b), in_=src.rearrange("c m n -> m c n"))
+        def load_r(i):
+            g0, g1, a, b = r_loads[i]
+            nc.sync.dma_start(out=res[i][:], in_=r[g0:g1, :, a:b].rearrange("c m n -> m c n"))
 
-        def interleave(e, dst, src):
-            d = dst.rearrange("p (c i) j -> p c j i", i=RUN)
-            v = src.rearrange("p j (c i) -> p c j i", i=RUN)
-            if e == "V":
-                nc.vector.tensor_copy(out=d, in_=v)
-            else:
-                nc.scalar.copy(out=d, in_=v)
+        def interleave(copy, dst, src):
+            copy(out=dst.rearrange("p (c i) j -> p c j i", i=RUN), in_=src.rearrange("p j (c i) -> p c j i", i=RUN))
 
-        def weave_x(e, s, a, b):
-            interleave(e, x_bf[s][:, a:b, :], xv(s, a, b))
+        on_vector, on_scalar = nc.vector.tensor_copy, nc.scalar.copy
 
-        def weave_w(e, s, z):
-            interleave(e, w_bf[s][:, z], w_raw[s][z][:])
+        def interleave_x(copy, pair, a, b, places=ALL):
+            interleave(copy, x_bf[pair][:, a:b, places[0] : places[1]], x_view(pair, a, b, places))
 
-        def quant_x(s, h, a=0, b=HALF):
-            cols = slice(HALF * h + a, HALF * h + b)
+        def interleave_w(copy, pair, mat):
+            interleave(copy, w_bf[pair][:, mat], w_raw[pair][mat][:])
+
+        def quantise_x(pair, a, b):
             nc.vector.quantize_mx(
-                out=x_code[s][:, cols].bitcast(FP8X4),
-                scales=x_scale[s][:, cols],
-                in_=x_bf[s][:, cols, :].rearrange("p n j -> p (n j)"),
+                out=x_code[pair][:, a:b].bitcast(FP8X4),
+                scales=x_scale[pair][:, a:b],
+                in_=x_bf[pair][:, a:b, :].rearrange("p n j -> p (n j)"),
             )
 
-        def quant_w(s, z):
-            outs = slice(M * z, M * (z + 1))
+        def quantise_w(pair, mat):
+            outs = slice(M * mat, M * (mat + 1))
             nc.vector.quantize_mx(
-                out=w_code[s][:, outs].bitcast(FP8X4),
-                scales=w_scale[s][:, outs],
-                in_=w_bf[s][:, z].rearrange("p m j -> p (m j)"),
+                out=w_code[pair][:, outs].bitcast(FP8X4),
+                scales=w_scale[pair][:, outs],
+                in_=w_bf[pair][:, mat].rearrange("p m j -> p (m j)"),
             )
 
-        def multiply(s, h, z, places=(0, 1)):
-            cols = slice(HALF * h, HALF * (h + 1))
-            outs = slice(M * z, M * (z + 1))
-            for c in places:
+        def multiply(pair, half, mat):
+            cols = slice(HALF * half, HALF * (half + 1))
+            outs = slice(M * mat, M * (mat + 1))
+            for c in range(SIDE):
                 rows = slice(ROWS * c, ROWS * (c + 1))
                 nc.tensor.matmul_mx(
-                    out=acc[h][c][z][:],
-                    lhsT=w_code[s][rows, outs].bitcast(FP8X4),
-                    lhsT_scale=w_scale[s][rows, outs],
-                    rhs=x_code[s][rows, cols].bitcast(FP8X4),
-                    rhs_scale=x_scale[s][rows, cols],
+                    out=acc[half][c][mat][:],
+                    lhsT=w_code[pair][rows, outs].bitcast(FP8X4),
+                    lhsT_scale=w_scale[pair][rows, outs],
+                    rhs=x_code[pair][rows, cols].bitcast(FP8X4),
+                    rhs_scale=x_scale[pair][rows, cols],
                     start=True,
                     stop=True,
                 )
 
-        def activate(s, h, c, a=0, b=HALF):
-            nc.scalar.activation(out=gate[s][:, c, HALF * h + a : HALF * h + b], in_=acc[h][c][0][:, a:b], func=ACT.Tanh)
+        def tanh(g, a, b):
+            pair, c = divmod(g, SIDE)
+            half, a_h = divmod(a, HALF)
+            nc.scalar.activation(out=gate[pair][:, c, a:b], in_=acc[half][c][0][:, a_h : a_h + b - a], func=ACT.Tanh)
 
-        def product(s, h, c, a=0, b=HALF):
-            t = gate[s][:, c, HALF * h + a : HALF * h + b]
-            nc.vector.tensor_tensor(out=t, in0=t, in1=acc[h][c][1][:, a:b], op=ALU.mult)
+        def product(g, a, b):
+            pair, c = divmod(g, SIDE)
+            half, a_h = divmod(a, HALF)
+            t = gate[pair][:, c, a:b]
+            nc.vector.tensor_tensor(out=t, in0=t, in1=acc[half][c][1][:, a_h : a_h + b - a], op=ALU.mult)
 
-        def residual(e, s, c0, c1, a, b):
-            eng = nc.vector if e == "V" else nc.gpsimd
-            t = rv(s, c0, c1, a, b)
-            eng.tensor_tensor(out=t, in0=gate[s][:, c0:c1, a:b], in1=t, op=ALU.add)
+        def add_r(engine, g, a, b):
+            pair, c = divmod(g, SIDE)
+            t = res_view(g, a, b)
+            engine.tensor_tensor(out=t, in0=gate[pair][:, c : c + 1, a:b], in1=t, op=ALU.add)
 
-        def store(queue, s, c0, c1, a, b):
-            dst = out[SIDE * s + c0 : SIDE * s + c1, :, a:b]
-            queue.dma_start(out=dst.rearrange("c m n -> m c n"), in_=rv(s, c0, c1, a, b))
+        def store(g, a, b):
+            nc.sync.dma_start(out=out[g : g + 1, :, a:b].rearrange("c m n -> m c n"), in_=res_view(g, a, b))
 
-        load_x(0, 0, 1024)
-        load_w(0, 0)
-        load_w(0, 1)
-        load_x(1, 0, 512)
-        load_w(1, 0)
-        load_w(1, 1)
-        load_r(0, 0, 1, 0, 1024)
-        load_x(1, 512, 768)
-        load_x(1, 768, 1024)
-        load_r(0, 1, 2, 0, 1024)
-        load_r(1, 0, 2, 0, 512)
-        load_r(1, 0, 2, 512, 1024)
-        weave_x("V", 0, 0, 352)
-        weave_x("S", 0, 352, 512)
-        weave_x("S", 0, 672, 1024)
-        weave_w("V", 0, 0)
-        quant_x(0, 0)
-        quant_w(0, 0)
+        load_x(0)
+        load_x(1)
+        load_weights(0)
+        load_x(2)
+        load_x(3)
+        load_weights(1)
+        load_r(0)
+        load_x(4)
+        load_x(5)
+        for i in range(1, len(r_loads)):
+            load_r(i)
+
+        interleave_x(on_vector, 0, 0, VECTOR_PART, LOW)
+        interleave_x(on_scalar, 0, VECTOR_PART, HALF, LOW)
+        interleave_x(on_vector, 0, HALF, HALF + EARLY_PART, LOW)
+        interleave_x(on_scalar, 0, HALF + VECTOR_PART, N, LOW)
+        interleave_x(on_vector, 0, 0, VECTOR_PART, HIGH)
+        interleave_x(on_scalar, 0, VECTOR_PART, HALF, HIGH)
+        interleave_w(on_vector, 0, 0)
+        quantise_x(0, 0, HALF)
+        quantise_w(0, 0)
         multiply(0, 0, 0)
-        weave_w("V", 0, 1)
-        weave_x("V", 0, 512, 672)
-        quant_w(0, 1)
+        interleave_w(on_scalar, 0, 1)
+        interleave_x(on_vector, 0, HALF + EARLY_PART, HALF + VECTOR_PART, LOW)
+        quantise_w(0, 1)
         multiply(0, 0, 1)
-        quant_x(0, 1)
+        interleave_x(on_vector, 0, HALF, HALF + VECTOR_PART, HIGH)
+        interleave_x(on_scalar, 0, HALF + VECTOR_PART, N, HIGH)
+        tanh(0, 0, HALF)
+        tanh(1, 0, HALF)
+        quantise_x(0, HALF, N)
         multiply(0, 1, 0)
         multiply(0, 1, 1)
-        activate(0, 0, 0)
-        activate(0, 0, 1)
-        weave_x("V", 1, 0, 256)
-        weave_x("V", 1, 256, 400)
-        weave_x("S", 1, 400, 512)
-        quant_x(1, 0, 0, 256)
-        product(0, 0, 1, 0, 256)
-        quant_x(1, 0, 256, 512)
-        weave_w("S", 1, 0)
-        product(0, 0, 1, 256, 512)
-        quant_w(1, 0)
+        product(0, 0, HALF - HELD)
+        product(1, 0, EARLY_PRODUCT)
+
+        interleave_x(on_vector, 1, 0, QUARTER)
+        interleave_x(on_vector, 1, QUARTER, MIDDLE_PART)
+        interleave_x(on_scalar, 1, MIDDLE_PART, HALF)
+        quantise_x(1, 0, QUARTER)
+        quantise_x(1, QUARTER, HALF)
+        interleave_w(on_scalar, 1, 0)
+        quantise_w(1, 0)
         multiply(1, 0, 0)
-        weave_w("S", 1, 1)
-        activate(0, 1, 0)
-        activate(0, 1, 1)
-        product(0, 0, 0)
-        quant_w(1, 1)
+        interleave_w(on_scalar, 1, 1)
+        tanh(0, HALF, N)
+        tanh(1, HALF, N)
+        product(1, EARLY_PRODUCT, HALF)
+        product(0, HALF - HELD, HALF)
+        quantise_w(1, 1)
         multiply(1, 0, 1)
-        residual("G", 0, 0, 1, 0, 512)
-        product(0, 1, 0)
-        residual("G", 0, 0, 1, 512, 768)
-        activate(1, 0, 0)
-        activate(1, 0, 1)
-        product(0, 1, 1)
-        product(1, 0, 0)
-        product(1, 0, 1, 0, 448)
-        residual("V", 0, 0, 1, 768, 1024)
-        weave_x("S", 1, 512, 768)
-        weave_x("V", 1, 768, 928)
-        weave_x("S", 1, 928, 1024)
-        quant_x(1, 1, 0, 256)
-        quant_x(1, 1, 256, 512)
+
+        add_r(nc.gpsimd, 0, 0, HALF)
+        product(0, HALF, N)
+        add_r(nc.gpsimd, 0, HALF, GPSIMD_END)
+        tanh(2, 0, HALF)
+        tanh(3, 0, HALF)
+        product(1, HALF, N)
+        product(2, 0, HALF)
+        product(3, 0, HALF - HELD)
+        add_r(nc.vector, 0, GPSIMD_END, N)
+
+        last = HALF + QUARTER
+        interleave_x(on_scalar, 1, HALF, last)
+        interleave_x(on_vector, 1, last, last + LAST_PART)
+        interleave_x(on_scalar, 1, last + LAST_PART, N)
+        quantise_x(1, HALF, last)
+        quantise_x(1, last, N)
         multiply(1, 1, 0)
         multiply(1, 1, 1)
-        activate(1, 1, 0, 0, 256)
-        activate(1, 1, 0, 256, 512)
-        activate(1, 1, 1, 0, 256)
-        activate(1, 1, 1, 256, 512)
-        residual("V", 0, 1, 2, 0, 1024)
-        product(1, 0, 1, 448, 512)
-        residual("V", 1, 0, 1, 0, 512)
-        residual("G", 1, 1, 2, 0, 512)
-        product(1, 1, 0, 0, 256)
-        product(1, 1, 0, 256, 512)
-        product(1, 1, 1, 0, 256)
-        product(1, 1, 1, 256, 512)
-        residual("V", 1, 0, 1, 512, 1024)
-        residual("V", 1, 1, 2, 512, 1024)
-        store(nc.sync, 0, 0, 1, 0, 1024)
-        store(nc.sync, 0, 1, 2, 0, 1024)
-        store(nc.sync, 1, 0, 1, 0, 512)
-        store(nc.sync, 1, 1, 2, 0, 512)
-        store(nc.sync, 1, 0, 1, 512, 1024)
-        store(nc.sync, 1, 1, 2, 512, 1024)
+
+        pieces = [(g, a, a + QUARTER) for g in (2, 3) for a in (HALF, last)]
+        for g, a, b in pieces:
+            tanh(g, a, b)
+        add_r(nc.vector, 1, 0, N)
+        product(3, HALF - HELD, HALF)
+        add_r(nc.vector, 2, 0, HALF)
+        add_r(nc.gpsimd, 3, 0, HALF)
+        for g, a, b in pieces:
+            product(g, a, b)
+        add_r(nc.vector, 2, HALF, N)
+        add_r(nc.vector, 3, HALF, N)
+
+        store(0, 0, N)
+        store(1, 0, N)
+        for a in (0, HALF):
+            store(2, a, a + HALF)
+            store(3, a, a + HALF)

@@ -41,7 +41,7 @@ def tile_rows_gglu_tanh_res_kernel(tc, x, w, u, r, out):
         ctx.enter_context(tc.manual_schedule())
 
         def per_pair(name, shape, dtype):
-            return [sb.tile(shape, dtype, name="%s%d" % (name, pair), align_bytes=64) for pair in range(PAIRS)]
+            return [sb.tile(shape, dtype, name="%s%d" % (name, pair), align_bytes=256) for pair in range(PAIRS)]
 
         x_loads = [
             (0, 0, N, LOW),
@@ -52,14 +52,14 @@ def tile_rows_gglu_tanh_res_kernel(tc, x, w, u, r, out):
             (1, HALF + QUARTER, N, ALL),
         ]
         x_raw = [
-            sb.tile([P, j1 - j0, b - a], F32, name="x_raw%d" % i, align_bytes=64)
+            sb.tile([P, j1 - j0, b - a], F32, name="x_raw%d" % i, align_bytes=256)
             for i, (pair, a, b, (j0, j1)) in enumerate(x_loads)
         ]
         x_bf = per_pair("x_bf", [P, N, PACK], BF16)
         x_code = per_pair("x_code", [P, N], U32)
         x_scale = per_pair("x_scale", [P, N], U8)
         w_raw = [
-            [sb.tile([P, PACK, M], F32, name="w_raw%d%d" % (pair, mat), align_bytes=64) for mat in range(2)]
+            [sb.tile([P, PACK, M], F32, name="w_raw%d%d" % (pair, mat), align_bytes=256) for mat in range(2)]
             for pair in range(PAIRS)
         ]
         w_bf = per_pair("w_bf", [P, 2, M, PACK], BF16)
@@ -67,7 +67,7 @@ def tile_rows_gglu_tanh_res_kernel(tc, x, w, u, r, out):
         w_scale = per_pair("w_scale", [P, 2 * M], U8)
         gate = per_pair("gate", [P, SIDE, N], F32)
         r_loads = [(0, 1, 0, N), (1, 2, 0, N), (2, 4, 0, HALF), (2, 4, HALF, N)]
-        res = [sb.tile([P, g1 - g0, b - a], F32, name="res%d" % i, align_bytes=64) for i, (g0, g1, a, b) in enumerate(r_loads)]
+        res = [sb.tile([P, g1 - g0, b - a], F32, name="res%d" % i, align_bytes=256) for i, (g0, g1, a, b) in enumerate(r_loads)]
         acc = [
             [[ps.tile([P, HALF], F32, name="acc%d%d%d" % (half, c, mat)) for mat in range(2)] for c in range(SIDE)]
             for half in range(2)

@@ -40,8 +40,8 @@ def tile_rows_gglu_tanh_res_kernel(tc, x, w, u, r, out):
         ps = ctx.enter_context(tc.psum_pool(name="ps", bufs=1))
         ctx.enter_context(tc.manual_schedule())
 
-        def per_pair(name, shape, dtype):
-            return [sb.tile(shape, dtype, name="%s%d" % (name, pair), align_bytes=256) for pair in range(PAIRS)]
+        def per_pair(name, shape, dtype, align=256):
+            return [sb.tile(shape, dtype, name="%s%d" % (name, pair), align_bytes=align) for pair in range(PAIRS)]
 
         x_loads = [
             (0, 0, N, LOW),
@@ -52,22 +52,22 @@ def tile_rows_gglu_tanh_res_kernel(tc, x, w, u, r, out):
             (1, HALF + QUARTER, N, ALL),
         ]
         x_raw = [
-            sb.tile([P, j1 - j0, b - a], F32, name="x_raw%d" % i, align_bytes=256)
+            sb.tile([P, j1 - j0, b - a], F32, name="x_raw%d" % i, align_bytes=4096)
             for i, (pair, a, b, (j0, j1)) in enumerate(x_loads)
         ]
         x_bf = per_pair("x_bf", [P, N, PACK], BF16)
         x_code = per_pair("x_code", [P, N], U32)
         x_scale = per_pair("x_scale", [P, N], U8)
         w_raw = [
-            [sb.tile([P, PACK, M], F32, name="w_raw%d%d" % (pair, mat), align_bytes=256) for mat in range(2)]
+            [sb.tile([P, PACK, M], F32, name="w_raw%d%d" % (pair, mat), align_bytes=2048) for mat in range(2)]
             for pair in range(PAIRS)
         ]
         w_bf = per_pair("w_bf", [P, 2, M, PACK], BF16)
         w_code = per_pair("w_code", [P, 2 * M], U32)
         w_scale = per_pair("w_scale", [P, 2 * M], U8)
-        gate = per_pair("gate", [P, SIDE, N], F32)
+        gate = per_pair("gate", [P, SIDE, N], F32, 4096)
         r_loads = [(0, 1, 0, N), (1, 2, 0, N), (2, 4, 0, HALF), (2, 4, HALF, N)]
-        res = [sb.tile([P, g1 - g0, b - a], F32, name="res%d" % i, align_bytes=256) for i, (g0, g1, a, b) in enumerate(r_loads)]
+        res = [sb.tile([P, g1 - g0, b - a], F32, name="res%d" % i, align_bytes=4096) for i, (g0, g1, a, b) in enumerate(r_loads)]
         acc = [
             [[ps.tile([P, HALF], F32, name="acc%d%d%d" % (half, c, mat)) for mat in range(2)] for c in range(SIDE)]
             for half in range(2)

@@ -30,7 +30,7 @@ MIDDLE_PART = 384
 LAST_PART = 160
 EARLY_PRODUCT = 320
 HELD = 64
-GPSIMD_END = HALF + QUARTER
+GPSIMD_START = 256
 
 
 def tile_rows_gglu_tanh_res_kernel(tc, x, w, u, r, out):
@@ -188,8 +188,8 @@ def tile_rows_gglu_tanh_res_kernel(tc, x, w, u, r, out):
         tanh(0, 0, HALF)
         tanh(1, 0, HALF)
         quantise_x(0, HALF, N)
-        multiply(0, 1, 0)
         multiply(0, 1, 1)
+        multiply(0, 1, 0)
         product(0, 0, HALF - HELD)
         product(1, 0, EARLY_PRODUCT)
 
@@ -209,15 +209,15 @@ def tile_rows_gglu_tanh_res_kernel(tc, x, w, u, r, out):
         quantise_w(1, 1)
         multiply(1, 0, 1)
 
-        add_r(nc.gpsimd, 0, 0, HALF)
+        add_r(nc.gpsimd, 0, GPSIMD_START, HALF)
         product(0, HALF, N)
-        add_r(nc.gpsimd, 0, HALF, GPSIMD_END)
+        add_r(nc.gpsimd, 0, HALF, N)
         tanh(2, 0, HALF)
         tanh(3, 0, HALF)
         product(1, HALF, N)
         product(2, 0, HALF)
-        product(3, 0, HALF - HELD)
-        add_r(nc.vector, 0, GPSIMD_END, N)
+        product(3, 0, HALF - 64)
+        add_r(nc.vector, 0, 0, GPSIMD_START)
 
         last = HALF + QUARTER
         interleave_x(on_scalar, 1, HALF, last)
@@ -232,7 +232,7 @@ def tile_rows_gglu_tanh_res_kernel(tc, x, w, u, r, out):
         for g, a, b in pieces:
             tanh(g, a, b)
         add_r(nc.vector, 1, 0, N)
-        product(3, HALF - HELD, HALF)
+        product(3, HALF - 64, HALF)
         add_r(nc.vector, 2, 0, HALF)
         add_r(nc.gpsimd, 3, 0, HALF)
         for g, a, b in pieces:

@@ -21,16 +21,7 @@ PAIRS = G // SIDE
 HALF = 512
 QUARTER = HALF // 2
 RUN = 2
-
 LOW, HIGH, ALL = (0, 2), (2, 4), (0, 4)
-
-VECTOR_PART = 352
-EARLY_PART = 192
-MIDDLE_PART = 384
-LAST_PART = 160
-EARLY_PRODUCT = 320
-HELD = 64
-GPSIMD_START = 256
 
 
 def tile_rows_gglu_tanh_res_kernel(tc, x, w, u, r, out):
@@ -43,14 +34,7 @@ def tile_rows_gglu_tanh_res_kernel(tc, x, w, u, r, out):
         def per_pair(name, shape, dtype, align=256):
             return [sb.tile(shape, dtype, name="%s%d" % (name, pair), align_bytes=align) for pair in range(PAIRS)]
 
-        x_loads = [
-            (0, 0, N, LOW),
-            (0, 0, HALF, HIGH),
-            (0, HALF, N, HIGH),
-            (1, 0, HALF, ALL),
-            (1, HALF, HALF + QUARTER, ALL),
-            (1, HALF + QUARTER, N, ALL),
-        ]
+        x_loads = [(0, 0, HALF, ALL), (0, HALF, 768, ALL), (0, 768, N, ALL), (1, 0, 256, ALL), (1, 256, HALF, ALL), (1, HALF, 768, ALL), (1, 768, N, ALL)]
         x_raw = [
             sb.tile([P, j1 - j0, b - a], F32, name="x_raw%d" % i, align_bytes=4096)
             for i, (pair, a, b, (j0, j1)) in enumerate(x_loads)
@@ -66,7 +50,7 @@ def tile_rows_gglu_tanh_res_kernel(tc, x, w, u, r, out):
         w_code = per_pair("w_code", [P, 2 * M], U32)
         w_scale = per_pair("w_scale", [P, 2 * M], U8)
         gate = per_pair("gate", [P, SIDE, N], F32, 4096)
-        r_loads = [(0, 1, 0, N), (1, 2, 0, N), (2, 4, 0, HALF), (2, 4, HALF, N)]
+        r_loads = [(0, 1, 0, 384), (0, 1, 384, N), (1, 2, 0, N), (2, 3, 0, HALF), (3, 4, 0, HALF), (2, 4, HALF, N)]
         res = [sb.tile([P, g1 - g0, b - a], F32, name="res%d" % i, align_bytes=4096) for i, (g0, g1, a, b) in enumerate(r_loads)]
         acc = [
             [[ps.tile([P, HALF], F32, name="acc%d%d%d" % (half, c, mat)) for mat in range(2)] for c in range(SIDE)]
@@ -88,10 +72,9 @@ def tile_rows_gglu_tanh_res_kernel(tc, x, w, u, r, out):
             src = x[SIDE * pair : SIDE * (pair + 1), :, a:b].rearrange("c (p j) n -> (c p) j n", j=PACK)
             nc.sync.dma_start(out=x_raw[i][:], in_=src[:, j0:j1, :])
 
-        def load_weights(pair):
-            for mat, weights in enumerate((w, u)):
-                src = weights[SIDE * pair : SIDE * (pair + 1)]
-                nc.sync.dma_start(out=w_raw[pair][mat][:], in_=src.rearrange("c (p j) m -> (c p) j m", j=PACK))
+        def load_w(pair, mat):
+            src = (w, u)[mat][SIDE * pair : SIDE * (pair + 1)]
+            nc.sync.dma_start(out=w_raw[pair][mat][:], in_=src.rearrange("c (p j) m -> (c p) j m", j=PACK))
 
         def load_r(i):
             g0, g1, a, b = r_loads[i]
@@ -157,78 +140,73 @@ def tile_rows_gglu_tanh_res_kernel(tc, x, w, u, r, out):
         def store(g, a, b):
             nc.sync.dma_start(out=out[g : g + 1, :, a:b].rearrange("c m n -> m c n"), in_=res_view(g, a, b))
 
+
         load_x(0)
+        load_w(0, 0)
+        load_w(0, 1)
         load_x(1)
-        load_weights(0)
         load_x(2)
         load_x(3)
-        load_weights(1)
-        load_r(0)
         load_x(4)
+        load_w(1, 0)
+        load_w(1, 1)
+        load_r(0)
+        load_r(1)
         load_x(5)
-        for i in range(1, len(r_loads)):
+        load_x(6)
+        for i in range(2, len(r_loads)):
             load_r(i)
-
-        interleave_x(on_vector, 0, 0, VECTOR_PART, LOW)
-        interleave_x(on_scalar, 0, VECTOR_PART, HALF, LOW)
-        interleave_x(on_vector, 0, HALF, HALF + EARLY_PART, LOW)
-        interleave_x(on_scalar, 0, HALF + VECTOR_PART, N, LOW)
-        interleave_x(on_vector, 0, 0, VECTOR_PART, HIGH)
-        interleave_x(on_scalar, 0, VECTOR_PART, HALF, HIGH)
+        interleave_x(on_vector, 0, 0, 352)
+        interleave_x(on_scalar, 0, 352, HALF)
         interleave_w(on_vector, 0, 0)
         quantise_x(0, 0, HALF)
         quantise_w(0, 0)
         multiply(0, 0, 0)
         interleave_w(on_scalar, 0, 1)
-        interleave_x(on_vector, 0, HALF + EARLY_PART, HALF + VECTOR_PART, LOW)
         quantise_w(0, 1)
         multiply(0, 0, 1)
-        interleave_x(on_vector, 0, HALF, HALF + VECTOR_PART, HIGH)
-        interleave_x(on_scalar, 0, HALF + VECTOR_PART, N, HIGH)
+        interleave_x(on_vector, 0, HALF, HALF + 160)
+        interleave_x(on_scalar, 0, HALF + 160, 768)
         tanh(0, 0, HALF)
         tanh(1, 0, HALF)
-        quantise_x(0, HALF, N)
-        multiply(0, 1, 1)
+        quantise_x(0, HALF, 768)
+        interleave_x(on_vector, 0, 768, N)
+        product(0, 0, HALF)
+        quantise_x(0, 768, N)
         multiply(0, 1, 0)
-        product(0, 0, HALF - HELD)
-        product(1, 0, EARLY_PRODUCT)
-
-        interleave_x(on_vector, 1, 0, QUARTER)
-        interleave_x(on_vector, 1, QUARTER, MIDDLE_PART)
-        interleave_x(on_scalar, 1, MIDDLE_PART, HALF)
-        quantise_x(1, 0, QUARTER)
-        quantise_x(1, QUARTER, HALF)
-        interleave_w(on_scalar, 1, 0)
+        multiply(0, 1, 1)
+        product(1, 0, HALF)
+        interleave_x(on_scalar, 1, 0, 256)
+        interleave_x(on_vector, 1, 256, 256 + 128)
+        interleave_x(on_scalar, 1, 256 + 128, HALF)
+        quantise_x(1, 0, 256)
+        interleave_w(on_vector, 1, 0)
+        quantise_x(1, 256, HALF)
         quantise_w(1, 0)
         multiply(1, 0, 0)
-        interleave_w(on_scalar, 1, 1)
         tanh(0, HALF, N)
+        interleave_w(on_scalar, 1, 1)
         tanh(1, HALF, N)
-        product(1, EARLY_PRODUCT, HALF)
-        product(0, HALF - HELD, HALF)
+        product(0, HALF, N - 64)
         quantise_w(1, 1)
         multiply(1, 0, 1)
-
-        add_r(nc.gpsimd, 0, GPSIMD_START, HALF)
-        product(0, HALF, N)
-        add_r(nc.gpsimd, 0, HALF, N)
+        product(0, N - 64, N)
+        add_r(nc.vector, 0, 0, 384)
+        add_r(nc.gpsimd, 0, 384, N)
+        product(1, HALF, N)
         tanh(2, 0, HALF)
         tanh(3, 0, HALF)
-        product(1, HALF, N)
         product(2, 0, HALF)
         product(3, 0, HALF - 64)
-        add_r(nc.vector, 0, 0, GPSIMD_START)
 
-        last = HALF + QUARTER
-        interleave_x(on_scalar, 1, HALF, last)
-        interleave_x(on_vector, 1, last, last + LAST_PART)
-        interleave_x(on_scalar, 1, last + LAST_PART, N)
-        quantise_x(1, HALF, last)
-        quantise_x(1, last, N)
+        interleave_x(on_scalar, 1, HALF, 768)
+        interleave_x(on_vector, 1, 768, 768 + 192)
+        interleave_x(on_scalar, 1, 768 + 192, N)
+        quantise_x(1, HALF, 768)
+        quantise_x(1, 768, N)
         multiply(1, 1, 0)
         multiply(1, 1, 1)
-
-        pieces = [(g, a, a + QUARTER) for g in (2, 3) for a in (HALF, last)]
+        pieces = [(g, a, a + QUARTER) for g in (2, 3) for a in (HALF, 768)]
         for g, a, b in pieces:
             tanh(g, a, b)
         add_r(nc.vector, 1, 0, N)
@@ -239,8 +217,8 @@ def tile_rows_gglu_tanh_res_kernel(tc, x, w, u, r, out):
             product(g, a, b)
         add_r(nc.vector, 2, HALF, N)
         add_r(nc.vector, 3, HALF, N)
-
-        store(0, 0, N)
+        store(0, 0, 384)
+        store(0, 384, N)
         store(1, 0, N)
         for a in (0, HALF):
             store(2, a, a + HALF)

@@ -34,7 +34,7 @@ def tile_rows_gglu_tanh_res_kernel(tc, x, w, u, r, out):
         def per_pair(name, shape, dtype, align=256):
             return [sb.tile(shape, dtype, name="%s%d" % (name, pair), align_bytes=align) for pair in range(PAIRS)]
 
-        x_loads = [(0, 0, HALF, ALL), (0, HALF, 768, ALL), (0, 768, N, ALL), (1, 0, 256, ALL), (1, 256, HALF, ALL), (1, HALF, 768, ALL), (1, 768, N, ALL)]
+        x_loads = [(0, 0, HALF, ALL), (0, HALF, N, LOW), (0, HALF, N, HIGH), (1, 0, 256, ALL), (1, 256, HALF, ALL), (1, HALF, 768, ALL), (1, 768, N, ALL)]
         x_raw = [
             sb.tile([P, j1 - j0, b - a], F32, name="x_raw%d" % i, align_bytes=4096)
             for i, (pair, a, b, (j0, j1)) in enumerate(x_loads)
@@ -50,8 +50,9 @@ def tile_rows_gglu_tanh_res_kernel(tc, x, w, u, r, out):
         w_code = per_pair("w_code", [P, 2 * M], U32)
         w_scale = per_pair("w_scale", [P, 2 * M], U8)
         gate = per_pair("gate", [P, SIDE, N], F32, 4096)
+        r_tiles = [(0, 1, 0, N), (1, 2, 0, N), (2, 4, 0, HALF), (2, 4, HALF, N)]
         r_loads = [(0, 1, 0, 384), (0, 1, 384, N), (1, 2, 0, N), (2, 3, 0, HALF), (3, 4, 0, HALF), (2, 4, HALF, N)]
-        res = [sb.tile([P, g1 - g0, b - a], F32, name="res%d" % i, align_bytes=4096) for i, (g0, g1, a, b) in enumerate(r_loads)]
+        res = [sb.tile([P, g1 - g0, b - a], F32, name="res%d" % i, align_bytes=4096) for i, (g0, g1, a, b) in enumerate(r_tiles)]
         acc = [
             [[ps.tile([P, HALF], F32, name="acc%d%d%d" % (half, c, mat)) for mat in range(2)] for c in range(SIDE)]
             for half in range(2)
@@ -62,10 +63,10 @@ def tile_rows_gglu_tanh_res_kernel(tc, x, w, u, r, out):
                 if (pair_l, places_l) == (pair, places) and a_l <= a and b <= b_l:
                     return loaded[:, :, a - a_l : b - a_l]
 
-        def res_view(g, a, b):
-            for loaded, (g0, g1, a_l, b_l) in zip(res, r_loads):
+        def res_view(g, a, b, groups=1):
+            for loaded, (g0, g1, a_l, b_l) in zip(res, r_tiles):
                 if g0 <= g < g1 and a_l <= a and b <= b_l:
-                    return loaded[:, g - g0 : g - g0 + 1, a - a_l : b - a_l]
+                    return loaded[:, g - g0 : g - g0 + groups, a - a_l : b - a_l]
 
         def load_x(i):
             pair, a, b, (j0, j1) = x_loads[i]
@@ -78,7 +79,7 @@ def tile_rows_gglu_tanh_res_kernel(tc, x, w, u, r, out):
 
         def load_r(i):
             g0, g1, a, b = r_loads[i]
-            nc.sync.dma_start(out=res[i][:], in_=r[g0:g1, :, a:b].rearrange("c m n -> m c n"))
+            nc.sync.dma_start(out=res_view(g0, a, b, g1 - g0), in_=r[g0:g1, :, a:b].rearrange("c m n -> m c n"))
 
         def interleave(copy, dst, src):
             copy(out=dst.rearrange("p (c i) j -> p c j i", i=RUN), in_=src.rearrange("p j (c i) -> p c j i", i=RUN))
@@ -140,7 +141,6 @@ def tile_rows_gglu_tanh_res_kernel(tc, x, w, u, r, out):
         def store(g, a, b):
             nc.sync.dma_start(out=out[g : g + 1, :, a:b].rearrange("c m n -> m c n"), in_=res_view(g, a, b))
 
-
         load_x(0)
         load_w(0, 0)
         load_w(0, 1)
@@ -165,18 +165,19 @@ def tile_rows_gglu_tanh_res_kernel(tc, x, w, u, r, out):
         interleave_w(on_scalar, 0, 1)
         quantise_w(0, 1)
         multiply(0, 0, 1)
-        interleave_x(on_vector, 0, HALF, HALF + 160)
-        interleave_x(on_scalar, 0, HALF + 160, 768)
+        interleave_x(on_vector, 0, HALF, HALF + 384, LOW)
+        interleave_x(on_scalar, 0, HALF + 384, N, LOW)
         tanh(0, 0, HALF)
+        interleave_x(on_vector, 0, HALF, HALF + 384, HIGH)
+        interleave_x(on_scalar, 0, HALF + 384, N, HIGH)
         tanh(1, 0, HALF)
-        quantise_x(0, HALF, 768)
-        interleave_x(on_vector, 0, 768, N)
         product(0, 0, HALF)
-        quantise_x(0, 768, N)
+        quantise_x(0, HALF, N)
         multiply(0, 1, 0)
         multiply(0, 1, 1)
         product(1, 0, HALF)
         interleave_x(on_scalar, 1, 0, 256)
+
         interleave_x(on_vector, 1, 256, 256 + 128)
         interleave_x(on_scalar, 1, 256 + 128, HALF)
         quantise_x(1, 0, 256)
@@ -187,6 +188,7 @@ def tile_rows_gglu_tanh_res_kernel(tc, x, w, u, r, out):
         tanh(0, HALF, N)
         interleave_w(on_scalar, 1, 1)
         tanh(1, HALF, N)
+
         product(0, HALF, N - 64)
         quantise_w(1, 1)
         multiply(1, 0, 1)
@@ -198,7 +200,6 @@ def tile_rows_gglu_tanh_res_kernel(tc, x, w, u, r, out):
         tanh(3, 0, HALF)
         product(2, 0, HALF)
         product(3, 0, HALF - 64)
-
         interleave_x(on_scalar, 1, HALF, 768)
         interleave_x(on_vector, 1, 768, 768 + 192)
         interleave_x(on_scalar, 1, 768 + 192, N)
@@ -217,8 +218,7 @@ def tile_rows_gglu_tanh_res_kernel(tc, x, w, u, r, out):
             product(g, a, b)
         add_r(nc.vector, 2, HALF, N)
         add_r(nc.vector, 3, HALF, N)
-        store(0, 0, 384)
-        store(0, 384, N)
+        store(0, 0, N)
         store(1, 0, N)
         for a in (0, HALF):
             store(2, a, a + HALF)

from contextlib import ExitStack

import concourse.mybir as mybir

G, D, M, N = 4, 256, 128, 1024
FLOPS = 2 * 2 * G * D * M * N

F32 = mybir.dt.float32
BF16 = mybir.dt.bfloat16
U32 = mybir.dt.uint32
U8 = mybir.dt.uint8
FP8X4 = mybir.dt.float8_e4m3fn_x4
ACT = mybir.ActivationFunctionType
ALU = mybir.AluOpType

P = 128
PACK = 4
ROWS = D // PACK
SIDE = P // ROWS
PAIRS = G // SIDE
HALF = 512
QUARTER = HALF // 2
RUN = 2
LOW, HIGH, ALL = (0, 2), (2, 4), (0, 4)


def tile_rows_gglu_tanh_res_kernel(tc, x, w, u, r, out):
    nc = tc.nc
    with ExitStack() as ctx:
        sb = ctx.enter_context(tc.tile_pool(name="sb", bufs=1))
        ps = ctx.enter_context(tc.psum_pool(name="ps", bufs=1))
        ctx.enter_context(tc.manual_schedule())

        def per_pair(name, shape, dtype, align=256):
            return [sb.tile(shape, dtype, name="%s%d" % (name, pair), align_bytes=align) for pair in range(PAIRS)]

        x_loads = [(0, 0, HALF, ALL), (0, HALF, N, LOW), (0, HALF, N, HIGH), (1, 0, 256, ALL), (1, 256, HALF, ALL), (1, HALF, 768, ALL), (1, 768, N, ALL)]
        x_raw = [
            sb.tile([P, j1 - j0, b - a], F32, name="x_raw%d" % i, align_bytes=4096)
            for i, (pair, a, b, (j0, j1)) in enumerate(x_loads)
        ]
        x_bf = per_pair("x_bf", [P, N, PACK], BF16)
        x_code = per_pair("x_code", [P, N], U32)
        x_scale = per_pair("x_scale", [P, N], U8)
        w_raw = [
            [sb.tile([P, PACK, M], F32, name="w_raw%d%d" % (pair, mat), align_bytes=2048) for mat in range(2)]
            for pair in range(PAIRS)
        ]
        w_bf = per_pair("w_bf", [P, 2, M, PACK], BF16)
        w_code = per_pair("w_code", [P, 2 * M], U32)
        w_scale = per_pair("w_scale", [P, 2 * M], U8)
        gate = per_pair("gate", [P, SIDE, N], F32, 4096)
        r_tiles = [(0, 1, 0, N), (1, 2, 0, N), (2, 4, 0, HALF), (2, 4, HALF, N)]
        r_loads = [(0, 1, 0, 384), (0, 1, 384, N), (1, 2, 0, N), (2, 3, 0, HALF), (3, 4, 0, HALF), (2, 4, HALF, N)]
        res = [sb.tile([P, g1 - g0, b - a], F32, name="res%d" % i, align_bytes=4096) for i, (g0, g1, a, b) in enumerate(r_tiles)]
        acc = [
            [[ps.tile([P, HALF], F32, name="acc%d%d%d" % (half, c, mat)) for mat in range(2)] for c in range(SIDE)]
            for half in range(2)
        ]

        def x_view(pair, a, b, places):
            for loaded, (pair_l, a_l, b_l, places_l) in zip(x_raw, x_loads):
                if (pair_l, places_l) == (pair, places) and a_l <= a and b <= b_l:
                    return loaded[:, :, a - a_l : b - a_l]

        def res_view(g, a, b, groups=1):
            for loaded, (g0, g1, a_l, b_l) in zip(res, r_tiles):
                if g0 <= g < g1 and a_l <= a and b <= b_l:
                    return loaded[:, g - g0 : g - g0 + groups, a - a_l : b - a_l]

        def load_x(i):
            pair, a, b, (j0, j1) = x_loads[i]
            src = x[SIDE * pair : SIDE * (pair + 1), :, a:b].rearrange("c (p j) n -> (c p) j n", j=PACK)
            nc.sync.dma_start(out=x_raw[i][:], in_=src[:, j0:j1, :])

        def load_w(pair, mat):
            src = (w, u)[mat][SIDE * pair : SIDE * (pair + 1)]
            nc.sync.dma_start(out=w_raw[pair][mat][:], in_=src.rearrange("c (p j) m -> (c p) j m", j=PACK))

        def load_r(i):
            g0, g1, a, b = r_loads[i]
            nc.sync.dma_start(out=res_view(g0, a, b, g1 - g0), in_=r[g0:g1, :, a:b].rearrange("c m n -> m c n"))

        def interleave(copy, dst, src):
            copy(out=dst.rearrange("p (c i) j -> p c j i", i=RUN), in_=src.rearrange("p j (c i) -> p c j i", i=RUN))

        on_vector, on_scalar = nc.vector.tensor_copy, nc.scalar.copy

        def interleave_x(copy, pair, a, b, places=ALL):
            interleave(copy, x_bf[pair][:, a:b, places[0] : places[1]], x_view(pair, a, b, places))

        def interleave_w(copy, pair, mat):
            interleave(copy, w_bf[pair][:, mat], w_raw[pair][mat][:])

        def quantise_x(pair, a, b):
            nc.vector.quantize_mx(
                out=x_code[pair][:, a:b].bitcast(FP8X4),
                scales=x_scale[pair][:, a:b],
                in_=x_bf[pair][:, a:b, :].rearrange("p n j -> p (n j)"),
            )

        def quantise_w(pair, mat):
            outs = slice(M * mat, M * (mat + 1))
            nc.vector.quantize_mx(
                out=w_code[pair][:, outs].bitcast(FP8X4),
                scales=w_scale[pair][:, outs],
                in_=w_bf[pair][:, mat].rearrange("p m j -> p (m j)"),
            )

        def multiply(pair, half, mat):
            cols = slice(HALF * half, HALF * (half + 1))
            outs = slice(M * mat, M * (mat + 1))
            for c in range(SIDE):
                rows = slice(ROWS * c, ROWS * (c + 1))
                nc.tensor.matmul_mx(
                    out=acc[half][c][mat][:],
                    lhsT=w_code[pair][rows, outs].bitcast(FP8X4),
                    lhsT_scale=w_scale[pair][rows, outs],
                    rhs=x_code[pair][rows, cols].bitcast(FP8X4),
                    rhs_scale=x_scale[pair][rows, cols],
                    start=True,
                    stop=True,
                )

        def tanh(g, a, b):
            pair, c = divmod(g, SIDE)
            half, a_h = divmod(a, HALF)
            nc.scalar.activation(out=gate[pair][:, c, a:b], in_=acc[half][c][0][:, a_h : a_h + b - a], func=ACT.Tanh)

        def product(g, a, b):
            pair, c = divmod(g, SIDE)
            half, a_h = divmod(a, HALF)
            t = gate[pair][:, c, a:b]
            nc.vector.tensor_tensor(out=t, in0=t, in1=acc[half][c][1][:, a_h : a_h + b - a], op=ALU.mult)

        def add_r(engine, g, a, b):
            pair, c = divmod(g, SIDE)
            t = res_view(g, a, b)
            engine.tensor_tensor(out=t, in0=gate[pair][:, c : c + 1, a:b], in1=t, op=ALU.add)

        def store(g, a, b):
            nc.sync.dma_start(out=out[g : g + 1, :, a:b].rearrange("c m n -> m c n"), in_=res_view(g, a, b))

        load_x(0)
        load_w(0, 0)
        load_w(0, 1)
        load_x(1)
        load_x(2)
        load_x(3)
        load_x(4)
        load_w(1, 0)
        load_w(1, 1)
        load_r(0)
        load_r(1)
        load_x(5)
        load_x(6)
        for i in range(2, len(r_loads)):
            load_r(i)
        interleave_x(on_vector, 0, 0, 352)
        interleave_x(on_scalar, 0, 352, HALF)
        interleave_w(on_vector, 0, 0)
        quantise_x(0, 0, HALF)
        quantise_w(0, 0)
        multiply(0, 0, 0)
        interleave_w(on_scalar, 0, 1)
        quantise_w(0, 1)
        multiply(0, 0, 1)
        interleave_x(on_vector, 0, HALF, HALF + 384, LOW)
        interleave_x(on_scalar, 0, HALF + 384, N, LOW)
        tanh(0, 0, HALF)
        interleave_x(on_vector, 0, HALF, HALF + 384, HIGH)
        interleave_x(on_scalar, 0, HALF + 384, N, HIGH)
        tanh(1, 0, HALF)
        product(0, 0, HALF)
        quantise_x(0, HALF, N)
        multiply(0, 1, 0)
        multiply(0, 1, 1)
        product(1, 0, HALF)
        interleave_x(on_scalar, 1, 0, 256)

        interleave_x(on_vector, 1, 256, 256 + 128)
        interleave_x(on_scalar, 1, 256 + 128, HALF)
        quantise_x(1, 0, 256)
        interleave_w(on_vector, 1, 0)
        quantise_x(1, 256, HALF)
        quantise_w(1, 0)
        multiply(1, 0, 0)
        tanh(0, HALF, N)
        interleave_w(on_scalar, 1, 1)
        tanh(1, HALF, N)

        product(0, HALF, N - 64)
        quantise_w(1, 1)
        multiply(1, 0, 1)
        product(0, N - 64, N)
        add_r(nc.vector, 0, 0, 384)
        add_r(nc.gpsimd, 0, 384, N)
        product(1, HALF, N)
        tanh(2, 0, HALF)
        tanh(3, 0, HALF)
        product(2, 0, HALF)
        product(3, 0, HALF - 64)
        interleave_x(on_scalar, 1, HALF, 768)
        interleave_x(on_vector, 1, 768, 768 + 192)
        interleave_x(on_scalar, 1, 768 + 192, N)
        quantise_x(1, HALF, 768)
        quantise_x(1, 768, N)
        multiply(1, 1, 0)
        multiply(1, 1, 1)
        pieces = [(g, a, a + QUARTER) for g in (2, 3) for a in (HALF, 768)]
        for g, a, b in pieces:
            tanh(g, a, b)
        add_r(nc.vector, 1, 0, N)
        product(3, HALF - 64, HALF)
        add_r(nc.vector, 2, 0, HALF)
        add_r(nc.gpsimd, 3, 0, HALF)
        for g, a, b in pieces:
            product(g, a, b)
        add_r(nc.vector, 2, HALF, N)
        add_r(nc.vector, 3, HALF, N)
        store(0, 0, N)
        store(1, 0, N)
        for a in (0, HALF):
            store(2, a, a + HALF)
            store(3, a, a + HALF)
